import numpy as np
import ml_dtypes


def mxq(x, axis, fmt="e4m3"):
    dtype, down = {"e4m3": (ml_dtypes.float8_e4m3fn, 7), "e5m2": (ml_dtypes.float8_e5m2, 14)}[fmt]
    v = np.moveaxis(np.asarray(x, np.float32).astype(ml_dtypes.bfloat16).astype(np.float64), axis, -1)
    blocks = v.reshape(v.shape[:-1] + (-1, 32))
    amax = np.abs(blocks).max(-1, keepdims=True)
    byte = np.maximum(np.where(amax > 0, np.frexp(amax)[1] - 1 + 127, 0) - down, 1)
    scale = np.exp2(byte - 127.0)
    codes = (blocks / scale).astype(np.float32).astype(dtype).astype(np.float64)
    return np.moveaxis((codes * scale).reshape(v.shape), -1, axis)


WIDE = False


def mx_kscale(k):
    if not WIDE:
        return np.ones(k)
    levels = np.array([30, -30])
    if k % 512:
        return np.exp2(np.random.permutation(np.resize(levels, k // 32))).repeat(32)
    a = np.empty((k // 512, 16))
    for p in range(k // 512):
        a[p, :8] = np.random.permutation(np.resize(levels, 8))
        for g in range(8):
            far = levels[np.abs(levels - a[p, g]) >= 10]
            a[p, g + 8] = far[np.random.randint(len(far))]
    return np.exp2(a.ravel()).repeat(32)


BF16 = ml_dtypes.bfloat16


def bf(x):
    return np.asarray(x, np.float32).astype(BF16)


def f64(x):
    return np.asarray(x).astype(np.float64)


E2M1 = np.array([0.0, 0.5, 1.0, 1.5, 2.0, 3.0, 4.0, 6.0, -0.0, -0.5, -1.0, -1.5, -2.0, -3.0, -4.0, -6.0])


def pack_weight(w, fmt):
    k, n = w.shape
    w = f64(bf(w)).reshape(k // 32, 32, n)
    amax = np.abs(w).max(1)
    if fmt == "e4m3":
        byte = np.frexp(amax)[1] - 1 + 127 - 7
    else:
        mant, ex = np.frexp(amax / 6.0)
        byte = np.where(mant > 0.5, ex, ex - 1) + 127
    byte = np.clip(np.where(amax > 0, byte, 1), 1, 254)
    scaled = (w * np.exp2(127.0 - byte)[:, None, :]).reshape(k, n).astype(np.float32)
    by_word = np.ascontiguousarray(scaled.reshape(k // 512, 128, 4, n).transpose(0, 1, 3, 2))
    if fmt == "e4m3":
        words = by_word.astype(ml_dtypes.float8_e4m3fn).view(np.uint8)
    else:
        c = by_word.astype(ml_dtypes.float4_e2m1fn).view(np.uint8) & 0xF
        words = c[..., 0::2] | (c[..., 1::2] << 4)
    return np.ascontiguousarray(words), np.ascontiguousarray(byte.astype(np.uint8).reshape(k // 512, 16, n))


def unpack_weight(words, scales, fmt):
    g, p, n, _ = words.shape
    if fmt == "e4m3":
        vals = np.ascontiguousarray(words).view(ml_dtypes.float8_e4m3fn).astype(np.float64)
    else:
        nib = np.empty((g, p, n, 4), np.uint8)
        nib[..., 0::2] = words & 0xF
        nib[..., 1::2] = words >> 4
        vals = E2M1[nib]
    vals = vals * np.repeat(np.exp2(scales.astype(np.float64) - 127.0), 8, axis=1)[..., None]
    return vals.transpose(0, 1, 3, 2).reshape(g * 512, n)
def pack4(w):
    words, scales = pack_weight(w, "e2m1")
    return words.reshape(words.shape[0], 128, -1), scales


def unpack4(words, scales):
    return unpack_weight(words.reshape(words.shape[0], 128, -1, 2), scales, "e2m1")


T, K, V, N = 1024, 2048, 1024, 512

FREQ_LOW, FREQ_HIGH = 0.01, 0.05
MEAN_DOSAGE = 0.06


def setup_inputs():
    s = mx_kscale(K)
    u = mx_kscale(V)
    freq = np.random.uniform(FREQ_LOW, FREQ_HIGH, V)
    dosage = np.random.binomial(2, freq, (K, V)) + 0.1 * np.abs(np.random.standard_normal((K, V)))
    dosage_words, dosage_scales = pack4(dosage / s[:, None])
    sd = np.exp(0.3 * np.random.standard_normal(T))
    resid = np.random.standard_normal((T, K)) * sd[:, None] / np.sqrt(MEAN_DOSAGE * K)
    weight = (1 - freq) ** 48
    member = np.random.exponential(1.0, (V, N)) ** 2 / V
    return {"resid": bf(resid * s),
            "dosage_words": dosage_words,
            "dosage_scales": dosage_scales,
            "weight": bf(weight * u),
            "member": bf(member / u[:, None]),
            "inv_var": bf(1 / sd ** 2)}


def reference(resid, dosage_words, dosage_scales, weight, member, inv_var):
    D = unpack4(dosage_words, dosage_scales)
    score = mxq(f64(resid), 1, "e4m3") @ D
    h = f64(weight) * np.square(score)
    stat = mxq(h, 1, "e5m2") @ mxq(f64(member), 0, "e4m3")
    return stat * f64(inv_var)[:, None]

@@ -1,0 +1,358 @@
+from contextlib import ExitStack
+
+import concourse.mybir as mybir
+from concourse.masks import make_identity
+
+T, K, V, N = 1024, 2048, 1024, 512
+
+FLOPS = 2 * T * K * V + 2 * T * V * N
+
+F32 = mybir.dt.float32
+BF16 = mybir.dt.bfloat16
+U32 = mybir.dt.uint32
+I32 = mybir.dt.int32
+U8 = mybir.dt.uint8
+E4M3X4 = mybir.dt.float8_e4m3fn_x4
+E5M2X4 = mybir.dt.float8_e5m2_x4
+E2M1X4 = mybir.dt.float4_e2m1fn_x4
+ACT = mybir.ActivationFunctionType
+ALU = mybir.AluOpType
+
+P = 128
+G = K // 512
+H = 2
+VG = 2
+
+
+def tile_skat_gene_scan_s9_kernel(tc, resid, dosage_words, dosage_scales, weight, member, inv_var, out):
+    nc = tc.nc
+    with ExitStack() as ctx:
+        keep = ctx.enter_context(tc.tile_pool(name="keep", bufs=1))
+        work = ctx.enter_context(tc.tile_pool(name="work", bufs=4))
+        outs = ctx.enter_context(tc.tile_pool(name="outs", bufs=8))
+        psum = ctx.enter_context(tc.psum_pool(name="psum", bufs=4))
+        ctx.enter_context(tc.manual_schedule())
+
+        def keep_tile(shape, dtype, name):
+            return keep.tile(shape, dtype, name=name, tag=name, align_bytes=64)
+
+        ident = keep_tile([P, P], F32, "ident")
+        sraw = keep_tile([P, G, V], U8, "sraw")
+        sperm = keep_tile([P, G * VG, 512], U8, "sperm")
+        wrow = keep_tile([P, P], BF16, "wrow")
+        wrow32 = keep_tile([P, P], F32, "wrow32")
+        wcol = keep_tile([P, 16], F32, "wcol")
+        sgn = keep_tile([P, 8], F32, "sgn")
+        sgn16 = keep_tile([P, 8], BF16, "sgn16")
+        absw = keep_tile([P, 8], F32, "absw")
+        root = keep_tile([P, 8], F32, "root")
+        rclamp = keep_tile([P, 8], F32, "rclamp")
+        rinv = keep_tile([P, 8], F32, "rinv")
+        quot = keep_tile([P, 8], F32, "quot")
+        rsum = keep_tile([P, 8], F32, "rsum")
+        rootw = keep_tile([P, 8], F32, "rootw")
+        dummy = keep_tile([P, 1], F32, "dummy")
+        draw = keep_tile([P, G, 2 * V], U8, "draw")
+        dperm = keep_tile([P, VG, G, 1024], U8, "dperm")
+        mraw = keep_tile([P, VG, 4, N], BF16, "mraw")
+        xr = {}
+        for h in range(H):
+            for g in range(G):
+                xr[h, g] = keep_tile([P, 4, 512], BF16, "xr%d%d" % (h, g))
+        rcode = {}
+        rscale = {}
+        for h in range(H):
+            for g in range(G):
+                rcode[h, g] = keep_tile([P, 512], U32, "rc%d%d" % (h, g))
+                rscale[h, g] = keep_tile([P, 512], U8, "rs%d%d" % (h, g))
+        hcode = {}
+        hscale = {}
+        for h in range(H):
+            for vg in range(VG):
+                hcode[h, vg] = keep_tile([P, 512], U32, "hc%d%d" % (h, vg))
+                hscale[h, vg] = keep_tile([P, 512], U8, "hs%d%d" % (h, vg))
+        mcode = [keep_tile([P, N], U32, "mc%d" % vg) for vg in range(VG)]
+        mscale = [keep_tile([P, N], U8, "ms%d" % vg) for vg in range(VG)]
+
+        nc.vector.memset(dummy[:], 0.0)
+        nc.scalar.activation(out=dummy[:], in_=dummy[:], func=ACT.Sqrt)
+        nc.vector.memset(sraw[:].rearrange("p g n -> p (g n)").bitcast(I32), 0)
+        nc.vector.memset(wrow[:], 0.0)
+        make_identity(nc, ident[:])
+
+        def load_x(h, g, lo, hi):
+            nc.sync.dma_start(
+                out=xr[h, g][:, lo:hi, :],
+                in_=resid[512 * h + 128 * lo : 512 * h + 128 * hi, 512 * g : 512 * (g + 1)].rearrange("(l p) k -> p l k", p=P),
+            )
+
+        words32 = dosage_words.bitcast(I32)
+        scales32 = dosage_scales.bitcast(I32)
+        sraw32 = sraw[:].rearrange("p g n -> p (g n)").bitcast(I32).rearrange("p (g n) -> p g n", g=G)
+        draw32 = draw[:].rearrange("p g n -> p (g n)").bitcast(I32).rearrange("p (g n) -> p g n", g=G)
+        wview = weight.rearrange("(v m t i) -> v t m i", v=VG, t=4, i=4)
+        for vg in range(VG):
+            nc.gpsimd.dma_start(
+                out=wrow[4 * vg : 4 * vg + 4, :].rearrange("t (m i) -> t m i", i=4), in_=wview[vg]
+            )
+        nc.gpsimd.dma_start(out=wrow[8:16, :], in_=inv_var.rearrange("(c p) -> c p", p=P))
+        for g in range(G):
+            if g == 0:
+                load_x(0, g, 0, 2)
+                load_x(0, g, 2, 4)
+            else:
+                load_x(0, g, 0, 4)
+            nc.sync.dma_start(out=draw32[:, g, :], in_=words32[g])
+            if g == 0:
+                for q in range(4):
+                    nc.scalar.dma_start(
+                        out=sraw32[32 * q : 32 * q + 4, :, :],
+                        in_=scales32[:, 4 * q : 4 * q + 4, :].rearrange("g r n -> r g n"),
+                    )
+        for g in range(G):
+            load_x(1, g, 0, 4)
+        mview = member.rearrange("(v m t i) w -> v i m t w", v=VG, t=4, i=4)
+        for vg in range(VG):
+            for i in range(4):
+                nc.sync.dma_start(out=mraw[i:P:4, vg, :, :], in_=mview[vg, i])
+
+        tbank = {}
+
+        def transposes(h, g):
+            flat = xr[h, g][:].rearrange("p l k -> p (l k)").bitcast(F32)
+            for pair in range(2):
+                bank = psum.tile([P, 2, 2, P], F32, name="tb", tag="tr")
+                tbank[h, g, pair] = bank
+                for l in range(2):
+                    for u in range(2):
+                        base = 256 * (2 * pair + l)
+                        nc.tensor.transpose(bank[:, l, u, :], flat[:, base + u : base + 256 : 2], ident[:])
+
+        xg = {}
+
+        def evacuate(h, g, pair, engine):
+            dst = work.tile([P, 256, 4], BF16, name="xg", tag="xg", bufs=8, align_bytes=64)
+            xg[h, g, pair] = dst
+            o = dst[:].rearrange("p r t -> p (r t)").bitcast(F32).rearrange("p (l r u) -> p l r u", l=2, u=2)
+            i = tbank[h, g, pair][:].rearrange("p l u r -> p l r u")
+            if engine == "S":
+                nc.scalar.copy(out=o, in_=i)
+            else:
+                nc.vector.tensor_copy(out=o, in_=i)
+
+        def quantize_x(h, g, pair):
+            cols = slice(256 * pair, 256 * (pair + 1))
+            nc.vector.quantize_mx(
+                out=rcode[h, g][:, cols].bitcast(E4M3X4),
+                scales=rscale[h, g][:, cols],
+                in_=xg[h, g, pair][:].rearrange("p r t -> p (r t)"),
+            )
+
+        def permute_d(vg, g):
+            dst = dperm[:, vg, g, :].bitcast(I32).rearrange("p (t m i) -> p t m i", t=4, i=2)
+            src = draw[:, g, 1024 * vg : 1024 * (vg + 1)].bitcast(I32).rearrange("p (m t i) -> p t m i", t=4, i=2)
+            nc.vector.tensor_copy(out=dst, in_=src)
+
+        def permute_scales():
+            src = sraw32.rearrange("p g n -> p (g n)").rearrange("p (c m t) -> p c t m", c=8, t=4)
+            dst = sperm[:].rearrange("p c n -> p (c n)").bitcast(I32).rearrange("p (c t m) -> p c t m", c=8, t=4)
+            nc.vector.tensor_copy(out=dst, in_=src)
+
+        acc = {}
+
+        def open_acc(h, vg):
+            for t in range(4):
+                bank = psum.tile([P, 512], F32, name="acc", tag="acc")
+                acc[h, vg, t] = bank
+
+        def stage1(h, vg, t, g):
+            nc.tensor.matmul_mx(
+                out=acc[h, vg, t][:],
+                lhsT=dperm[:, vg, g, 256 * t : 256 * (t + 1)].bitcast(E2M1X4),
+                lhsT_scale=sperm[:, VG * g + vg, 128 * t : 128 * (t + 1)],
+                rhs=rcode[h, g][:].bitcast(E4M3X4),
+                rhs_scale=rscale[h, g][:],
+                start=(g == 0),
+                stop=(g == G - 1),
+            )
+
+        hsq = {}
+
+        def square(h, vg, t):
+            if t == 0:
+                sq = work.tile([P, 4, 512], BF16, name="hsq", tag="hsq", bufs=2, align_bytes=64)
+                hsq[h, vg] = sq
+            nc.scalar.activation(
+                out=hsq[h, vg][:, t, :],
+                in_=acc[h, vg, t][:],
+                func=ACT.Square,
+                scale=rootw[:, 4 * vg + t : 4 * vg + t + 1],
+            )
+
+        hg = {}
+
+        def interleave_h(h, vg, lo, hi):
+            dst = work.tile([P, hi - lo, 4], BF16, name="hg", tag="hg%d" % (hi - lo), bufs=2, align_bytes=64)
+            hg[h, vg, lo] = dst
+            nc.vector.tensor_copy(out=dst[:], in_=hsq[h, vg][:, :, lo:hi].rearrange("p t r -> p r t"))
+
+        def quantize_h(h, vg, lo, hi):
+            nc.vector.quantize_mx(
+                out=hcode[h, vg][:, lo:hi].bitcast(E5M2X4),
+                scales=hscale[h, vg][:, lo:hi],
+                in_=hg[h, vg, lo][:].rearrange("p r t -> p (r t)"),
+            )
+
+        mg = {}
+
+        def interleave_m(vg):
+            dst = work.tile([P, N, 4], BF16, name="mg", tag="mg", bufs=2, align_bytes=64)
+            mg[vg] = dst
+            nc.vector.tensor_tensor(
+                out=dst[:],
+                in0=mraw[:, vg, :, :].rearrange("p t w -> p w t"),
+                in1=sgn16[:, 4 * vg : 4 * vg + 4].unsqueeze(1).to_broadcast([P, N, 4]),
+                op=ALU.mult,
+            )
+
+        def quantize_m(vg):
+            nc.vector.quantize_mx(
+                out=mcode[vg][:].bitcast(E4M3X4),
+                scales=mscale[vg][:],
+                in_=mg[vg][:].rearrange("p w t -> p (w t)"),
+            )
+
+        obank = {}
+
+        def stage2(h, l, vg):
+            if vg == 0:
+                bank = psum.tile([P, N], F32, name="ob", tag="tr" if h == 0 else "acc")
+                obank[h, l] = bank
+            cols = slice(128 * l, 128 * (l + 1))
+            nc.tensor.matmul_mx(
+                out=obank[h, l][:],
+                lhsT=hcode[h, vg][:, cols].bitcast(E5M2X4),
+                lhsT_scale=hscale[h, vg][:, cols],
+                rhs=mcode[vg][:].bitcast(E4M3X4),
+                rhs_scale=mscale[vg][:],
+                start=(vg == 0),
+                stop=(vg == VG - 1),
+            )
+
+        def store(h, l, engine):
+            o = outs.tile([P, N], F32, name="o", tag="o", align_bytes=64)
+            tile_no = 4 * h + l
+            factor = wcol[:, 8 + tile_no : 9 + tile_no]
+            if engine == "S":
+                nc.scalar.activation(out=o[:], in_=obank[h, l][:], func=ACT.Copy, scale=factor)
+            else:
+                nc.vector.tensor_scalar(out=o[:], in0=obank[h, l][:], scalar1=factor, scalar2=None, op0=ALU.mult)
+            nc.sync.dma_start(out=out[128 * tile_no : 128 * (tile_no + 1), :], in_=o[:])
+
+        def weight_columns():
+            nc.vector.tensor_copy(out=wrow32[:], in_=wrow[:])
+            bank = psum.tile([P, 512], F32, name="wb", tag="tr")
+            nc.tensor.transpose(bank[:, 0:P], wrow32[:], ident[:])
+            nc.vector.tensor_copy(out=wcol[:], in_=bank[:, 0:16])
+            w = wcol[:, 0:8]
+            nc.gpsimd.tensor_scalar(out=sgn[:], in0=w, scalar1=0.0, scalar2=2.0, op0=ALU.is_ge, op1=ALU.mult)
+            nc.gpsimd.tensor_scalar(out=sgn[:], in0=sgn[:], scalar1=1.0, scalar2=-1.0, op0=ALU.mult, op1=ALU.add)
+            nc.gpsimd.tensor_tensor(out=absw[:], in0=w, in1=sgn[:], op=ALU.mult)
+            nc.gpsimd.tensor_copy(out=sgn16[:], in_=sgn[:])
+
+        def weight_roots():
+            nc.scalar.activation(out=root[:], in_=absw[:], func=ACT.Sqrt)
+            nc.gpsimd.tensor_scalar(out=rclamp[:], in0=root[:], scalar1=1e-30, scalar2=None, op0=ALU.max)
+
+        def refine_roots():
+            nc.vector.reciprocal(out=rinv[:], in_=rclamp[:])
+            nc.gpsimd.tensor_tensor(out=quot[:], in0=absw[:], in1=rinv[:], op=ALU.mult)
+            nc.gpsimd.tensor_tensor(out=rsum[:], in0=root[:], in1=quot[:], op=ALU.add)
+            nc.gpsimd.tensor_scalar(out=rootw[:], in0=rsum[:], scalar1=0.5, scalar2=0.0, op0=ALU.mult, op1=ALU.add)
+
+        open_acc(0, 0)
+        transposes(0, 0)
+        evacuate(0, 0, 0, "S")
+        evacuate(0, 0, 1, "V")
+        permute_d(0, 0)
+        for g in range(G):
+            if g + 1 < G:
+                transposes(0, g + 1)
+            quantize_x(0, g, 0)
+            quantize_x(0, g, 1)
+            if g == 0:
+                permute_scales()
+            if g == 1:
+                weight_columns()
+            for t in range(4):
+                stage1(0, 0, t, g)
+            if g + 1 < G:
+                evacuate(0, g + 1, 0, "S")
+                evacuate(0, g + 1, 1, "V")
+                permute_d(0, g + 1)
+            if g == 2:
+                weight_roots()
+        refine_roots()
+
+        transposes(1, 0)
+        transposes(1, 1)
+        for g in range(G):
+            permute_d(1, g)
+        for t in range(4):
+            square(0, 0, t)
+        for g in range(2):
+            for pair in range(2):
+                evacuate(1, g, pair, "S")
+        open_acc(0, 1)
+        for t in range(2):
+            for g in range(G):
+                stage1(0, 1, t, g)
+            square(0, 1, t)
+        interleave_h(0, 0, 0, 512)
+        for g in range(2):
+            for pair in range(2):
+                quantize_x(1, g, pair)
+        quantize_h(0, 0, 0, 512)
+        transposes(1, 2)
+        transposes(1, 3)
+        for g in range(2, 4):
+            evacuate(1, g, 0, "S")
+            evacuate(1, g, 1, "V")
+        for g in range(2, 4):
+            for pair in range(2):
+                quantize_x(1, g, pair)
+        for t in range(2, 4):
+            for g in range(G):
+                stage1(0, 1, t, g)
+            square(0, 1, t)
+        interleave_h(0, 1, 0, 512)
+        quantize_h(0, 1, 0, 512)
+
+        for vg in range(VG):
+            open_acc(1, vg)
+            for t in range(4):
+                for g in range(G):
+                    stage1(1, vg, t, g)
+                square(1, vg, t)
+            if vg == 0:
+                interleave_m(0)
+                interleave_m(1)
+                quantize_m(0)
+                quantize_m(1)
+                interleave_h(1, 0, 0, 512)
+                quantize_h(1, 0, 0, 512)
+
+        for l in range(4):
+            for vg in range(VG):
+                stage2(0, l, vg)
+        interleave_h(1, 1, 0, 256)
+        interleave_h(1, 1, 256, 512)
+        quantize_h(1, 1, 0, 256)
+        quantize_h(1, 1, 256, 512)
+        for l in range(4):
+            store(0, l, "S")
+        for l in range(4):
+            stage2(1, l, 0)
+        for l in range(4):
+            stage2(1, l, 1)
+            store(1, l, "V" if l % 2 else "S")

@@ -74,9 +74,9 @@ def tile_skat_gene_scan_s9_kernel(tc, resid, dosage_words, dosage_scales, weight
         mcode = [keep_tile([P, N], U32, "mc%d" % vg) for vg in range(VG)]
         mscale = [keep_tile([P, N], U8, "ms%d" % vg) for vg in range(VG)]
 
+        nc.vector.memset(sraw[:].rearrange("p g n -> p (g n)").bitcast(I32), 0)
         nc.vector.memset(dummy[:], 0.0)
         nc.scalar.activation(out=dummy[:], in_=dummy[:], func=ACT.Sqrt)
-        nc.vector.memset(sraw[:].rearrange("p g n -> p (g n)").bitcast(I32), 0)
         nc.vector.memset(wrow[:], 0.0)
         make_identity(nc, ident[:])
 
@@ -90,25 +90,30 @@ def tile_skat_gene_scan_s9_kernel(tc, resid, dosage_words, dosage_scales, weight
         scales32 = dosage_scales.bitcast(I32)
         sraw32 = sraw[:].rearrange("p g n -> p (g n)").bitcast(I32).rearrange("p (g n) -> p g n", g=G)
         draw32 = draw[:].rearrange("p g n -> p (g n)").bitcast(I32).rearrange("p (g n) -> p g n", g=G)
+        def load_d(vg, lo, hi):
+            cols = slice(256 * vg, 256 * (vg + 1))
+            nc.sync.dma_start(out=draw32[:, lo:hi, cols], in_=words32[lo:hi, :, cols].rearrange("g p n -> p g n"))
+
+        load_x(0, 0, 0, 2)
+        load_x(0, 0, 2, 4)
+        for q in range(4):
+            nc.sync.dma_start(
+                out=sraw32[32 * q : 32 * q + 4, :, :],
+                in_=scales32[:, 4 * q : 4 * q + 4, :].rearrange("g r n -> r g n"),
+            )
+        load_d(0, 0, 1)
+        load_x(0, 1, 0, 4)
+        load_d(0, 1, 2)
         wview = weight.rearrange("(v m t i) -> v t m i", v=VG, t=4, i=4)
         for vg in range(VG):
-            nc.gpsimd.dma_start(
+            nc.sync.dma_start(
                 out=wrow[4 * vg : 4 * vg + 4, :].rearrange("t (m i) -> t m i", i=4), in_=wview[vg]
             )
-        nc.gpsimd.dma_start(out=wrow[8:16, :], in_=inv_var.rearrange("(c p) -> c p", p=P))
-        for g in range(G):
-            if g == 0:
-                load_x(0, g, 0, 2)
-                load_x(0, g, 2, 4)
-            else:
-                load_x(0, g, 0, 4)
-            nc.sync.dma_start(out=draw32[:, g, :], in_=words32[g])
-            if g == 0:
-                for q in range(4):
-                    nc.scalar.dma_start(
-                        out=sraw32[32 * q : 32 * q + 4, :, :],
-                        in_=scales32[:, 4 * q : 4 * q + 4, :].rearrange("g r n -> r g n"),
-                    )
+        nc.sync.dma_start(out=wrow[8:16, :], in_=inv_var.rearrange("(c p) -> c p", p=P))
+        for g in range(2, G):
+            load_x(0, g, 0, 4)
+            load_d(0, g, g + 1)
+        load_d(1, 0, 4)
         for g in range(G):
             load_x(1, g, 0, 4)
         mview = member.rearrange("(v m t i) w -> v i m t w", v=VG, t=4, i=4)
@@ -116,36 +121,44 @@ def tile_skat_gene_scan_s9_kernel(tc, resid, dosage_words, dosage_scales, weight
             for i in range(4):
                 nc.sync.dma_start(out=mraw[i:P:4, vg, :, :], in_=mview[vg, i])
 
+        xs = {}
+
+        def reorder_x(h, g, lo, hi):
+            if lo == 0:
+                tile = work.tile([P, 4, 2, P], F32, name="xs", tag="xs", bufs=4, align_bytes=64)
+                xs[h, g] = tile
+            src = xr[h, g][:, lo:hi, :].rearrange("p l k -> p (l k)").bitcast(F32)
+            nc.vector.tensor_copy(out=xs[h, g][:, lo:hi, :, :], in_=src.rearrange("p (l i u) -> p l u i", u=2, i=P))
+
         tbank = {}
 
         def transposes(h, g):
-            flat = xr[h, g][:].rearrange("p l k -> p (l k)").bitcast(F32)
             for pair in range(2):
                 bank = psum.tile([P, 2, 2, P], F32, name="tb", tag="tr")
                 tbank[h, g, pair] = bank
                 for l in range(2):
                     for u in range(2):
-                        base = 256 * (2 * pair + l)
-                        nc.tensor.transpose(bank[:, l, u, :], flat[:, base + u : base + 256 : 2], ident[:])
+                        nc.tensor.transpose(bank[:, l, u, :], xs[h, g][:, 2 * pair + l, u, :], ident[:])
 
         xg = {}
 
         def evacuate(h, g, pair, engine):
-            dst = work.tile([P, 256, 4], BF16, name="xg", tag="xg", bufs=8, align_bytes=64)
-            xg[h, g, pair] = dst
-            o = dst[:].rearrange("p r t -> p (r t)").bitcast(F32).rearrange("p (l r u) -> p l r u", l=2, u=2)
+            if pair == 0:
+                tile = work.tile([P, 512, 4], BF16, name="xg", tag="xg", bufs=4, align_bytes=64)
+                xg[h, g] = tile
+            cols = xg[h, g][:, 256 * pair : 256 * (pair + 1), :]
+            o = cols.rearrange("p r t -> p (r t)").bitcast(F32).rearrange("p (l r u) -> p l r u", l=2, u=2)
             i = tbank[h, g, pair][:].rearrange("p l u r -> p l r u")
             if engine == "S":
                 nc.scalar.copy(out=o, in_=i)
             else:
                 nc.vector.tensor_copy(out=o, in_=i)
 
-        def quantize_x(h, g, pair):
-            cols = slice(256 * pair, 256 * (pair + 1))
+        def quantize_x(h, g, lo, hi):
             nc.vector.quantize_mx(
-                out=rcode[h, g][:, cols].bitcast(E4M3X4),
-                scales=rscale[h, g][:, cols],
-                in_=xg[h, g, pair][:].rearrange("p r t -> p (r t)"),
+                out=rcode[h, g][:, lo:hi].bitcast(E4M3X4),
+                scales=rscale[h, g][:, lo:hi],
+                in_=xg[h, g][:, lo:hi, :].rearrange("p r t -> p (r t)"),
             )
 
         def permute_d(vg, g):
@@ -271,56 +284,63 @@ def tile_skat_gene_scan_s9_kernel(tc, resid, dosage_words, dosage_scales, weight
             nc.gpsimd.tensor_scalar(out=rootw[:], in0=rsum[:], scalar1=0.5, scalar2=0.0, op0=ALU.mult, op1=ALU.add)
 
         open_acc(0, 0)
+        reorder_x(0, 0, 0, 2)
+        reorder_x(0, 0, 2, 4)
         transposes(0, 0)
         evacuate(0, 0, 0, "S")
-        evacuate(0, 0, 1, "V")
+        evacuate(0, 0, 1, "S")
+        permute_scales()
         permute_d(0, 0)
         for g in range(G):
             if g + 1 < G:
+                reorder_x(0, g + 1, 0, 4)
                 transposes(0, g + 1)
-            quantize_x(0, g, 0)
-            quantize_x(0, g, 1)
-            if g == 0:
-                permute_scales()
+                evacuate(0, g + 1, 0, "S")
+                evacuate(0, g + 1, 1, "S")
+            quantize_x(0, g, 0, 256)
+            quantize_x(0, g, 256, 512)
+            if g + 1 < G:
+                permute_d(0, g + 1)
             if g == 1:
                 weight_columns()
-            for t in range(4):
-                stage1(0, 0, t, g)
-            if g + 1 < G:
-                evacuate(0, g + 1, 0, "S")
-                evacuate(0, g + 1, 1, "V")
-                permute_d(0, g + 1)
             if g == 2:
                 weight_roots()
+            for t in range(4):
+                stage1(0, 0, t, g)
         refine_roots()
 
+        reorder_x(1, 0, 0, 4)
+        reorder_x(1, 1, 0, 4)
         transposes(1, 0)
         transposes(1, 1)
         for g in range(G):
             permute_d(1, g)
-        for t in range(4):
-            square(0, 0, t)
-        for g in range(2):
-            for pair in range(2):
-                evacuate(1, g, pair, "S")
+        square(0, 0, 0)
+        square(0, 0, 1)
+        evacuate(1, 0, 0, "S")
+        evacuate(1, 0, 1, "S")
+        square(0, 0, 2)
+        square(0, 0, 3)
+        evacuate(1, 1, 0, "S")
+        evacuate(1, 1, 1, "S")
+        reorder_x(1, 2, 0, 4)
+        reorder_x(1, 3, 0, 4)
         open_acc(0, 1)
         for t in range(2):
             for g in range(G):
                 stage1(0, 1, t, g)
             square(0, 1, t)
         interleave_h(0, 0, 0, 512)
-        for g in range(2):
-            for pair in range(2):
-                quantize_x(1, g, pair)
+        quantize_x(1, 0, 0, 512)
+        quantize_x(1, 1, 0, 512)
         quantize_h(0, 0, 0, 512)
         transposes(1, 2)
         transposes(1, 3)
         for g in range(2, 4):
             evacuate(1, g, 0, "S")
-            evacuate(1, g, 1, "V")
+            evacuate(1, g, 1, "S")
         for g in range(2, 4):
-            for pair in range(2):
-                quantize_x(1, g, pair)
+            quantize_x(1, g, 0, 512)
         for t in range(2, 4):
             for g in range(G):
                 stage1(0, 1, t, g)

@@ -22,6 +22,9 @@ P = 128
 G = K // 512
 H = 2
 VG = 2
+R0 = ["NNNN", "NNNN"]
+R1 = "VVVV"
+EV = {(0, 0): "SS", (0, 1): "SS", (1, 0): "SS", (1, 1): "SS"}
 
 
 def tile_skat_gene_scan_s9_kernel(tc, resid, dosage_words, dosage_scales, weight, member, inv_var, out):
@@ -49,16 +52,13 @@ def tile_skat_gene_scan_s9_kernel(tc, resid, dosage_words, dosage_scales, weight
         rclamp = keep_tile([P, 8], F32, "rclamp")
         rinv = keep_tile([P, 8], F32, "rinv")
         quot = keep_tile([P, 8], F32, "quot")
-        rsum = keep_tile([P, 8], F32, "rsum")
         rootw = keep_tile([P, 8], F32, "rootw")
         dummy = keep_tile([P, 1], F32, "dummy")
         draw = keep_tile([P, G, 2 * V], U8, "draw")
         dperm = keep_tile([P, VG, G, 1024], U8, "dperm")
         mraw = keep_tile([P, VG, 4, N], BF16, "mraw")
-        xr = {}
-        for h in range(H):
-            for g in range(G):
-                xr[h, g] = keep_tile([P, 4, 512], BF16, "xr%d%d" % (h, g))
+        x0 = [keep_tile([P, 4, 1024], BF16, "x0%d" % k) for k in range(2)]
+        x1 = [keep_tile([P, 2048], BF16, "x1%d" % l) for l in range(4)]
         rcode = {}
         rscale = {}
         for h in range(H):
@@ -75,15 +75,14 @@ def tile_skat_gene_scan_s9_kernel(tc, resid, dosage_words, dosage_scales, weight
         mscale = [keep_tile([P, N], U8, "ms%d" % vg) for vg in range(VG)]
 
         nc.vector.memset(sraw[:].rearrange("p g n -> p (g n)").bitcast(I32), 0)
-        nc.vector.memset(dummy[:], 0.0)
-        nc.scalar.activation(out=dummy[:], in_=dummy[:], func=ACT.Sqrt)
         nc.vector.memset(wrow[:], 0.0)
+        nc.vector.memset(dummy[:], 0.0)
         make_identity(nc, ident[:])
 
-        def load_x(h, g, lo, hi):
+        def load_x0(k, lo, hi):
             nc.sync.dma_start(
-                out=xr[h, g][:, lo:hi, :],
-                in_=resid[512 * h + 128 * lo : 512 * h + 128 * hi, 512 * g : 512 * (g + 1)].rearrange("(l p) k -> p l k", p=P),
+                out=x0[k][:, lo:hi, :],
+                in_=resid[128 * lo : 128 * hi, 1024 * k : 1024 * (k + 1)].rearrange("(l p) k -> p l k", p=P),
             )
 
         words32 = dosage_words.bitcast(I32)
@@ -94,57 +93,80 @@ def tile_skat_gene_scan_s9_kernel(tc, resid, dosage_words, dosage_scales, weight
             cols = slice(256 * vg, 256 * (vg + 1))
             nc.sync.dma_start(out=draw32[:, lo:hi, cols], in_=words32[lo:hi, :, cols].rearrange("g p n -> p g n"))
 
-        load_x(0, 0, 0, 2)
-        load_x(0, 0, 2, 4)
         for q in range(4):
-            nc.sync.dma_start(
+            nc.gpsimd.dma_start(
                 out=sraw32[32 * q : 32 * q + 4, :, :],
                 in_=scales32[:, 4 * q : 4 * q + 4, :].rearrange("g r n -> r g n"),
             )
-        load_d(0, 0, 1)
-        load_x(0, 1, 0, 4)
-        load_d(0, 1, 2)
+        load_x0(0, 0, 1)
+        load_x0(0, 1, 2)
         wview = weight.rearrange("(v m t i) -> v t m i", v=VG, t=4, i=4)
         for vg in range(VG):
             nc.sync.dma_start(
                 out=wrow[4 * vg : 4 * vg + 4, :].rearrange("t (m i) -> t m i", i=4), in_=wview[vg]
             )
         nc.sync.dma_start(out=wrow[8:16, :], in_=inv_var.rearrange("(c p) -> c p", p=P))
-        for g in range(2, G):
-            load_x(0, g, 0, 4)
-            load_d(0, g, g + 1)
+        load_x0(0, 2, 4)
+        load_d(0, 0, 2)
+        load_x0(1, 0, 2)
+        load_x0(1, 2, 4)
+        load_d(0, 2, 4)
         load_d(1, 0, 4)
-        for g in range(G):
-            load_x(1, g, 0, 4)
+        for l in range(4):
+            nc.sync.dma_start(out=x1[l][:], in_=resid[512 + 128 * l : 640 + 128 * l, :])
         mview = member.rearrange("(v m t i) w -> v i m t w", v=VG, t=4, i=4)
         for vg in range(VG):
             for i in range(4):
                 nc.sync.dma_start(out=mraw[i:P:4, vg, :, :], in_=mview[vg, i])
+        nc.scalar.activation(out=dummy[:], in_=dummy[:], func=ACT.Sqrt)
 
         xs = {}
 
-        def reorder_x(h, g, lo, hi):
-            if lo == 0:
-                tile = work.tile([P, 4, 2, P], F32, name="xs", tag="xs", bufs=4, align_bytes=64)
-                xs[h, g] = tile
-            src = xr[h, g][:, lo:hi, :].rearrange("p l k -> p (l k)").bitcast(F32)
-            nc.vector.tensor_copy(out=xs[h, g][:, lo:hi, :, :], in_=src.rearrange("p (l i u) -> p l u i", u=2, i=P))
+        def reorder_x0(k, l):
+            if R0[k][l] == "N":
+                flat = x0[k][:, l, :].bitcast(F32)
+                xs[0, l, k] = flat
+                return
+            tile = work.tile([P, 2, 2, P], F32, name="xs0", tag="xs0", bufs=8, align_bytes=64)
+            xs[0, l, k] = tile
+            src = x0[k][:, l, :].bitcast(F32)
+            cp = nc.vector.tensor_copy if R0[k][l] == "V" else nc.scalar.copy
+            cp(out=tile[:], in_=src.rearrange("p (g i u) -> p g u i", u=2, i=P))
+
+        def reorder_x1(l):
+            if R1[l] == "N":
+                flat = x1[l][:].bitcast(F32)
+                xs[1, l, 0] = flat[:, 0:512]
+                xs[1, l, 1] = flat[:, 512:1024]
+                return
+            tile = work.tile([P, 4, 2, P], F32, name="xs1", tag="xs1", bufs=4, align_bytes=64)
+            src = x1[l][:].bitcast(F32)
+            cp = nc.vector.tensor_copy if R1[l] == "V" else nc.scalar.copy
+            cp(out=tile[:], in_=src.rearrange("p (g i u) -> p g u i", u=2, i=P))
+            xs[1, l, 0] = tile[:, 0:2, :, :]
+            xs[1, l, 1] = tile[:, 2:4, :, :]
 
         tbank = {}
 
-        def transposes(h, g):
-            for pair in range(2):
+        def transposes(h, k, pair):
+            for g in (2 * k, 2 * k + 1):
                 bank = psum.tile([P, 2, 2, P], F32, name="tb", tag="tr")
                 tbank[h, g, pair] = bank
-                for l in range(2):
+            for l in range(2):
+                for g in (2 * k, 2 * k + 1):
                     for u in range(2):
-                        nc.tensor.transpose(bank[:, l, u, :], xs[h, g][:, 2 * pair + l, u, :], ident[:])
+                        s = xs[h, 2 * pair + l, k]
+                        if len(s.shape) == 2:
+                            s = s[:, 256 * (g % 2) + u : 256 * (g % 2) + 256 : 2]
+                        else:
+                            s = s[:, g % 2, u, :]
+                        nc.tensor.transpose(tbank[h, g, pair][:, l, u, :], s, ident[:])
 
         xg = {}
 
         def evacuate(h, g, pair, engine):
             if pair == 0:
-                tile = work.tile([P, 512, 4], BF16, name="xg", tag="xg", bufs=4, align_bytes=64)
+                tile = work.tile([P, 512, 4], BF16, name="xg", tag="xg", bufs=8, align_bytes=64)
                 xg[h, g] = tile
             cols = xg[h, g][:, 256 * pair : 256 * (pair + 1), :]
             o = cols.rearrange("p r t -> p (r t)").bitcast(F32).rearrange("p (l r u) -> p l r u", l=2, u=2)
@@ -262,85 +284,91 @@ def tile_skat_gene_scan_s9_kernel(tc, resid, dosage_words, dosage_scales, weight
                 nc.vector.tensor_scalar(out=o[:], in0=obank[h, l][:], scalar1=factor, scalar2=None, op0=ALU.mult)
             nc.sync.dma_start(out=out[128 * tile_no : 128 * (tile_no + 1), :], in_=o[:])
 
-        def weight_columns():
+        def weight_transpose():
             nc.vector.tensor_copy(out=wrow32[:], in_=wrow[:])
             bank = psum.tile([P, 512], F32, name="wb", tag="tr")
             nc.tensor.transpose(bank[:, 0:P], wrow32[:], ident[:])
             nc.vector.tensor_copy(out=wcol[:], in_=bank[:, 0:16])
-            w = wcol[:, 0:8]
-            nc.gpsimd.tensor_scalar(out=sgn[:], in0=w, scalar1=0.0, scalar2=2.0, op0=ALU.is_ge, op1=ALU.mult)
-            nc.gpsimd.tensor_scalar(out=sgn[:], in0=sgn[:], scalar1=1.0, scalar2=-1.0, op0=ALU.mult, op1=ALU.add)
-            nc.gpsimd.tensor_tensor(out=absw[:], in0=w, in1=sgn[:], op=ALU.mult)
-            nc.gpsimd.tensor_copy(out=sgn16[:], in_=sgn[:])
 
         def weight_roots():
+            w = wcol[:, 0:8]
+            nc.vector.scalar_tensor_tensor(out=absw[:], in0=w, scalar=-1.0, in1=w, op0=ALU.mult, op1=ALU.max)
+            nc.vector.tensor_scalar(out=sgn[:], in0=w, scalar1=0.0, scalar2=2.0, op0=ALU.is_ge, op1=ALU.mult)
             nc.scalar.activation(out=root[:], in_=absw[:], func=ACT.Sqrt)
-            nc.gpsimd.tensor_scalar(out=rclamp[:], in0=root[:], scalar1=1e-30, scalar2=None, op0=ALU.max)
 
         def refine_roots():
+            nc.vector.tensor_scalar(out=rclamp[:], in0=root[:], scalar1=1e-20, scalar2=None, op0=ALU.max)
+            nc.vector.tensor_scalar(out=sgn16[:], in0=sgn[:], scalar1=1.0, scalar2=None, op0=ALU.subtract)
             nc.vector.reciprocal(out=rinv[:], in_=rclamp[:])
-            nc.gpsimd.tensor_tensor(out=quot[:], in0=absw[:], in1=rinv[:], op=ALU.mult)
-            nc.gpsimd.tensor_tensor(out=rsum[:], in0=root[:], in1=quot[:], op=ALU.add)
-            nc.gpsimd.tensor_scalar(out=rootw[:], in0=rsum[:], scalar1=0.5, scalar2=0.0, op0=ALU.mult, op1=ALU.add)
+            nc.vector.scalar_tensor_tensor(out=quot[:], in0=rinv[:], scalar=0.5, in1=absw[:], op0=ALU.mult, op1=ALU.mult)
+            nc.vector.scalar_tensor_tensor(out=rootw[:], in0=root[:], scalar=0.5, in1=quot[:], op0=ALU.mult, op1=ALU.add)
+
+        def evacuate_pair(h, k, pair):
+            for g in (2 * k, 2 * k + 1):
+                evacuate(h, g, pair, EV[h, pair][g % 2])
 
         open_acc(0, 0)
-        reorder_x(0, 0, 0, 2)
-        reorder_x(0, 0, 2, 4)
-        transposes(0, 0)
-        evacuate(0, 0, 0, "S")
-        evacuate(0, 0, 1, "S")
+        for k in range(2):
+            for l in range(4):
+                reorder_x0(k, l)
+        transposes(0, 0, 0)
+        evacuate_pair(0, 0, 0)
+        weight_transpose()
+        weight_roots()
+        transposes(0, 0, 1)
+        evacuate_pair(0, 0, 1)
+        quantize_x(0, 0, 0, 256)
+        refine_roots()
+        quantize_x(0, 1, 0, 256)
         permute_scales()
         permute_d(0, 0)
-        for g in range(G):
-            if g + 1 < G:
-                reorder_x(0, g + 1, 0, 4)
-                transposes(0, g + 1)
-                evacuate(0, g + 1, 0, "S")
-                evacuate(0, g + 1, 1, "S")
-            quantize_x(0, g, 0, 256)
-            quantize_x(0, g, 256, 512)
-            if g + 1 < G:
-                permute_d(0, g + 1)
-            if g == 1:
-                weight_columns()
-            if g == 2:
-                weight_roots()
-            for t in range(4):
+        transposes(0, 1, 0)
+        evacuate_pair(0, 1, 0)
+        quantize_x(0, 0, 256, 512)
+        permute_d(0, 1)
+        quantize_x(0, 1, 256, 512)
+        for t in range(4):
+            stage1(0, 0, t, 0)
+        transposes(0, 1, 1)
+        evacuate_pair(0, 1, 1)
+        for t in range(4):
+            stage1(0, 0, t, 1)
+        quantize_x(0, 2, 0, 256)
+        quantize_x(0, 3, 0, 256)
+        permute_d(0, 2)
+        permute_d(0, 3)
+        quantize_x(0, 2, 256, 512)
+        quantize_x(0, 3, 256, 512)
+        reorder_x1(0)
+        reorder_x1(1)
+        for t in range(4):
+            for g in range(2, 4):
                 stage1(0, 0, t, g)
-        refine_roots()
+            square(0, 0, t)
 
-        reorder_x(1, 0, 0, 4)
-        reorder_x(1, 1, 0, 4)
-        transposes(1, 0)
-        transposes(1, 1)
         for g in range(G):
             permute_d(1, g)
-        square(0, 0, 0)
-        square(0, 0, 1)
-        evacuate(1, 0, 0, "S")
-        evacuate(1, 0, 1, "S")
-        square(0, 0, 2)
-        square(0, 0, 3)
-        evacuate(1, 1, 0, "S")
-        evacuate(1, 1, 1, "S")
-        reorder_x(1, 2, 0, 4)
-        reorder_x(1, 3, 0, 4)
         open_acc(0, 1)
+        transposes(1, 0, 0)
+        transposes(1, 1, 0)
+        evacuate_pair(1, 0, 0)
+        evacuate_pair(1, 1, 0)
+        reorder_x1(2)
+        reorder_x1(3)
         for t in range(2):
             for g in range(G):
                 stage1(0, 1, t, g)
             square(0, 1, t)
         interleave_h(0, 0, 0, 512)
-        quantize_x(1, 0, 0, 512)
-        quantize_x(1, 1, 0, 512)
+        for g in range(G):
+            quantize_x(1, g, 0, 256)
         quantize_h(0, 0, 0, 512)
-        transposes(1, 2)
-        transposes(1, 3)
-        for g in range(2, 4):
-            evacuate(1, g, 0, "S")
-            evacuate(1, g, 1, "S")
-        for g in range(2, 4):
-            quantize_x(1, g, 0, 512)
+        transposes(1, 0, 1)
+        transposes(1, 1, 1)
+        evacuate_pair(1, 0, 1)
+        evacuate_pair(1, 1, 1)
+        for g in range(G):
+            quantize_x(1, g, 256, 512)
         for t in range(2, 4):
             for g in range(G):
                 stage1(0, 1, t, g)
@@ -348,19 +376,25 @@ def tile_skat_gene_scan_s9_kernel(tc, resid, dosage_words, dosage_scales, weight
         interleave_h(0, 1, 0, 512)
         quantize_h(0, 1, 0, 512)
 
-        for vg in range(VG):
-            open_acc(1, vg)
+        open_acc(1, 0)
+        for g in range(2):
             for t in range(4):
-                for g in range(G):
-                    stage1(1, vg, t, g)
-                square(1, vg, t)
-            if vg == 0:
-                interleave_m(0)
-                interleave_m(1)
-                quantize_m(0)
-                quantize_m(1)
-                interleave_h(1, 0, 0, 512)
-                quantize_h(1, 0, 0, 512)
+                stage1(1, 0, t, g)
+        for t in range(4):
+            for g in range(2, 4):
+                stage1(1, 0, t, g)
+            square(1, 0, t)
+        interleave_m(0)
+        interleave_m(1)
+        quantize_m(0)
+        quantize_m(1)
+        interleave_h(1, 0, 0, 512)
+        quantize_h(1, 0, 0, 512)
+        open_acc(1, 1)
+        for t in range(4):
+            for g in range(G):
+                stage1(1, 1, t, g)
+            square(1, 1, t)
 
         for l in range(4):
             for vg in range(VG):

@@ -24,6 +24,7 @@ H = 2
 VG = 2
 R0 = ["NNNN", "NNNN"]
 R1 = "VVVV"
+WARM = 4
 EV = {(0, 0): "SS", (0, 1): "SS", (1, 0): "SS", (1, 1): "SS"}
 
 
@@ -54,6 +55,11 @@ def tile_skat_gene_scan_s9_kernel(tc, resid, dosage_words, dosage_scales, weight
         quot = keep_tile([P, 8], F32, "quot")
         rootw = keep_tile([P, 8], F32, "rootw")
         dummy = keep_tile([P, 1], F32, "dummy")
+        warm = keep_tile([P, 2048], BF16, "warm")
+        warm4 = keep_tile([P, 512], U32, "warm4")
+        warm4s = keep_tile([P, 512], U8, "warm4s")
+        warm5 = keep_tile([P, 128], U32, "warm5")
+        warm5s = keep_tile([P, 128], U8, "warm5s")
         draw = keep_tile([P, G, 2 * V], U8, "draw")
         dperm = keep_tile([P, VG, G, 1024], U8, "dperm")
         mraw = keep_tile([P, VG, 4, N], BF16, "mraw")
@@ -77,6 +83,9 @@ def tile_skat_gene_scan_s9_kernel(tc, resid, dosage_words, dosage_scales, weight
         nc.vector.memset(sraw[:].rearrange("p g n -> p (g n)").bitcast(I32), 0)
         nc.vector.memset(wrow[:], 0.0)
         nc.vector.memset(dummy[:], 0.0)
+        nc.gpsimd.memset(warm[:].bitcast(I32), 0)
+        nc.vector.quantize_mx(out=warm5[:].bitcast(E5M2X4), scales=warm5s[:], in_=warm[:, 0:512])
+        nc.vector.quantize_mx(out=warm4[:].bitcast(E4M3X4), scales=warm4s[:], in_=warm[:])
         make_identity(nc, ident[:])
 
         def load_x0(k, lo, hi):
@@ -94,21 +103,20 @@ def tile_skat_gene_scan_s9_kernel(tc, resid, dosage_words, dosage_scales, weight
             nc.sync.dma_start(out=draw32[:, lo:hi, cols], in_=words32[lo:hi, :, cols].rearrange("g p n -> p g n"))
 
         for q in range(4):
-            nc.gpsimd.dma_start(
+            nc.scalar.dma_start(
                 out=sraw32[32 * q : 32 * q + 4, :, :],
                 in_=scales32[:, 4 * q : 4 * q + 4, :].rearrange("g r n -> r g n"),
             )
-        load_x0(0, 0, 1)
-        load_x0(0, 1, 2)
+        load_x0(0, 0, 2)
+        load_x0(0, 2, 4)
+        load_d(0, 0, 2)
+        load_x0(1, 0, 2)
         wview = weight.rearrange("(v m t i) -> v t m i", v=VG, t=4, i=4)
         for vg in range(VG):
             nc.sync.dma_start(
                 out=wrow[4 * vg : 4 * vg + 4, :].rearrange("t (m i) -> t m i", i=4), in_=wview[vg]
             )
         nc.sync.dma_start(out=wrow[8:16, :], in_=inv_var.rearrange("(c p) -> c p", p=P))
-        load_x0(0, 2, 4)
-        load_d(0, 0, 2)
-        load_x0(1, 0, 2)
         load_x0(1, 2, 4)
         load_d(0, 2, 4)
         load_d(1, 0, 4)
@@ -288,7 +296,10 @@ def tile_skat_gene_scan_s9_kernel(tc, resid, dosage_words, dosage_scales, weight
             nc.vector.tensor_copy(out=wrow32[:], in_=wrow[:])
             bank = psum.tile([P, 512], F32, name="wb", tag="tr")
             nc.tensor.transpose(bank[:, 0:P], wrow32[:], ident[:])
-            nc.vector.tensor_copy(out=wcol[:], in_=bank[:, 0:16])
+            tbank["w"] = bank
+
+        def weight_copy():
+            nc.vector.tensor_copy(out=wcol[:], in_=tbank["w"][:, 0:16])
 
         def weight_roots():
             w = wcol[:, 0:8]
@@ -308,17 +319,28 @@ def tile_skat_gene_scan_s9_kernel(tc, resid, dosage_words, dosage_scales, weight
                 evacuate(h, g, pair, EV[h, pair][g % 2])
 
         open_acc(0, 0)
+
+        def warm_up(passes):
+            for i in range(passes):
+                nc.tensor.matmul_mx(
+                    out=acc[0, 0, 0][:],
+                    lhsT=warm5[:].bitcast(E5M2X4),
+                    lhsT_scale=warm5s[:],
+                    rhs=warm4[:].bitcast(E4M3X4),
+                    rhs_scale=warm4s[:],
+                    start=True,
+                    stop=True,
+                )
+
+        warm_up(WARM)
         for k in range(2):
             for l in range(4):
                 reorder_x0(k, l)
         transposes(0, 0, 0)
         evacuate_pair(0, 0, 0)
-        weight_transpose()
-        weight_roots()
         transposes(0, 0, 1)
         evacuate_pair(0, 0, 1)
         quantize_x(0, 0, 0, 256)
-        refine_roots()
         quantize_x(0, 1, 0, 256)
         permute_scales()
         permute_d(0, 0)
@@ -329,14 +351,18 @@ def tile_skat_gene_scan_s9_kernel(tc, resid, dosage_words, dosage_scales, weight
         quantize_x(0, 1, 256, 512)
         for t in range(4):
             stage1(0, 0, t, 0)
-        transposes(0, 1, 1)
-        evacuate_pair(0, 1, 1)
-        for t in range(4):
-            stage1(0, 0, t, 1)
+        weight_transpose()
         quantize_x(0, 2, 0, 256)
         quantize_x(0, 3, 0, 256)
         permute_d(0, 2)
         permute_d(0, 3)
+        weight_copy()
+        weight_roots()
+        transposes(0, 1, 1)
+        evacuate_pair(0, 1, 1)
+        refine_roots()
+        for t in range(4):
+            stage1(0, 0, t, 1)
         quantize_x(0, 2, 256, 512)
         quantize_x(0, 3, 256, 512)
         reorder_x1(0)
@@ -373,8 +399,12 @@ def tile_skat_gene_scan_s9_kernel(tc, resid, dosage_words, dosage_scales, weight
             for g in range(G):
                 stage1(0, 1, t, g)
             square(0, 1, t)
+        interleave_m(0)
         interleave_h(0, 1, 0, 512)
+        quantize_m(0)
+        interleave_m(1)
         quantize_h(0, 1, 0, 512)
+        quantize_m(1)
 
         open_acc(1, 0)
         for g in range(2):
@@ -384,10 +414,6 @@ def tile_skat_gene_scan_s9_kernel(tc, resid, dosage_words, dosage_scales, weight
             for g in range(2, 4):
                 stage1(1, 0, t, g)
             square(1, 0, t)
-        interleave_m(0)
-        interleave_m(1)
-        quantize_m(0)
-        quantize_m(1)
         interleave_h(1, 0, 0, 512)
         quantize_h(1, 0, 0, 512)
         open_acc(1, 1)
@@ -395,15 +421,19 @@ def tile_skat_gene_scan_s9_kernel(tc, resid, dosage_words, dosage_scales, weight
             for g in range(G):
                 stage1(1, 1, t, g)
             square(1, 1, t)
+            if t in (1, 2):
+                for vg in range(VG):
+                    stage2(0, t - 1, vg)
+                store(0, t - 1, "S")
 
-        for l in range(4):
+        for l in range(2, 4):
             for vg in range(VG):
                 stage2(0, l, vg)
         interleave_h(1, 1, 0, 256)
         interleave_h(1, 1, 256, 512)
         quantize_h(1, 1, 0, 256)
         quantize_h(1, 1, 256, 512)
-        for l in range(4):
+        for l in range(2, 4):
             store(0, l, "S")
         for l in range(4):
             stage2(1, l, 0)

@@ -25,7 +25,25 @@ VG = 2
 R0 = ["NNNN", "NNNN"]
 R1 = "VVVV"
 WARM = 4
-EV = {(0, 0): "SS", (0, 1): "SS", (1, 0): "SS", (1, 1): "SS"}
+D1 = 0
+D2 = 0
+MID = 1
+S2O = 0
+LATE = 3
+TP = (256, 256)
+E3 = "V"
+E2 = "SV"
+PD = 0
+WP = 0
+RP = 0
+SC = 1
+EV = {(0, 0, 0): "SS", (0, 0, 1): "SS", (0, 1, 0): "SS", (0, 1, 1): "SS", (1, 0, 0): "SS", (1, 0, 1): "SS", (1, 1, 0): "SS", (1, 1, 1): "SS"}
+WEAVE = {2: (0, 1)}
+EARLY = 1
+TAIL = 1
+LOADS = 2
+SPLIT = 2
+TS = "SSSS"
 
 
 def tile_skat_gene_scan_s9_kernel(tc, resid, dosage_words, dosage_scales, weight, member, inv_var, out):
@@ -43,9 +61,12 @@ def tile_skat_gene_scan_s9_kernel(tc, resid, dosage_words, dosage_scales, weight
         ident = keep_tile([P, P], F32, "ident")
         sraw = keep_tile([P, G, V], U8, "sraw")
         sperm = keep_tile([P, G * VG, 512], U8, "sperm")
-        wrow = keep_tile([P, P], BF16, "wrow")
-        wrow32 = keep_tile([P, P], F32, "wrow32")
-        wcol = keep_tile([P, 16], F32, "wcol")
+        wraw = keep_tile([P, P], BF16, "wraw")
+        wslot = keep_tile([P, P], BF16, "wslot")
+        wturn = keep_tile([P, P], BF16, "wturn")
+        vraw = keep_tile([P, 256], BF16, "vraw")
+        vturn = keep_tile([P, 256], BF16, "vturn")
+        vcol = keep_tile([P, 8], F32, "vcol")
         sgn = keep_tile([P, 8], F32, "sgn")
         sgn16 = keep_tile([P, 8], BF16, "sgn16")
         absw = keep_tile([P, 8], F32, "absw")
@@ -55,7 +76,7 @@ def tile_skat_gene_scan_s9_kernel(tc, resid, dosage_words, dosage_scales, weight
         quot = keep_tile([P, 8], F32, "quot")
         rootw = keep_tile([P, 8], F32, "rootw")
         dummy = keep_tile([P, 1], F32, "dummy")
-        warm = keep_tile([P, 2048], BF16, "warm")
+        warm = keep_tile([P, 512], BF16, "warm")
         warm4 = keep_tile([P, 512], U32, "warm4")
         warm4s = keep_tile([P, 512], U8, "warm4s")
         warm5 = keep_tile([P, 128], U32, "warm5")
@@ -80,12 +101,15 @@ def tile_skat_gene_scan_s9_kernel(tc, resid, dosage_words, dosage_scales, weight
         mcode = [keep_tile([P, N], U32, "mc%d" % vg) for vg in range(VG)]
         mscale = [keep_tile([P, N], U8, "ms%d" % vg) for vg in range(VG)]
 
+        nc.vector.memset(warm[:].bitcast(I32), 0)
+        nc.gpsimd.memset(warm4[:, 128:512], 0)
+        nc.gpsimd.memset(warm4s[:, 128:512].bitcast(I32), 0)
         nc.vector.memset(sraw[:].rearrange("p g n -> p (g n)").bitcast(I32), 0)
-        nc.vector.memset(wrow[:], 0.0)
         nc.vector.memset(dummy[:], 0.0)
-        nc.gpsimd.memset(warm[:].bitcast(I32), 0)
-        nc.vector.quantize_mx(out=warm5[:].bitcast(E5M2X4), scales=warm5s[:], in_=warm[:, 0:512])
-        nc.vector.quantize_mx(out=warm4[:].bitcast(E4M3X4), scales=warm4s[:], in_=warm[:])
+        nc.vector.quantize_mx(out=warm5[:].bitcast(E5M2X4), scales=warm5s[:], in_=warm[:])
+        nc.vector.quantize_mx(out=warm4[:, 0:128].bitcast(E4M3X4), scales=warm4s[:, 0:128], in_=warm[:])
+        nc.vector.memset(wraw[:].bitcast(I32), 0)
+        nc.vector.memset(vraw[:].bitcast(I32), 0)
         make_identity(nc, ident[:])
 
         def load_x0(k, lo, hi):
@@ -99,33 +123,90 @@ def tile_skat_gene_scan_s9_kernel(tc, resid, dosage_words, dosage_scales, weight
         sraw32 = sraw[:].rearrange("p g n -> p (g n)").bitcast(I32).rearrange("p (g n) -> p g n", g=G)
         draw32 = draw[:].rearrange("p g n -> p (g n)").bitcast(I32).rearrange("p (g n) -> p g n", g=G)
         def load_d(vg, lo, hi):
-            cols = slice(256 * vg, 256 * (vg + 1))
+            cols = slice(256 * vg, 256 * (vg + 1)) if vg < 2 else slice(0, 512)
             nc.sync.dma_start(out=draw32[:, lo:hi, cols], in_=words32[lo:hi, :, cols].rearrange("g p n -> p g n"))
 
-        for q in range(4):
-            nc.scalar.dma_start(
-                out=sraw32[32 * q : 32 * q + 4, :, :],
-                in_=scales32[:, 4 * q : 4 * q + 4, :].rearrange("g r n -> r g n"),
-            )
-        load_x0(0, 0, 2)
-        load_x0(0, 2, 4)
-        load_d(0, 0, 2)
-        load_x0(1, 0, 2)
-        wview = weight.rearrange("(v m t i) -> v t m i", v=VG, t=4, i=4)
-        for vg in range(VG):
-            nc.sync.dma_start(
-                out=wrow[4 * vg : 4 * vg + 4, :].rearrange("t (m i) -> t m i", i=4), in_=wview[vg]
-            )
-        nc.sync.dma_start(out=wrow[8:16, :], in_=inv_var.rearrange("(c p) -> c p", p=P))
-        load_x0(1, 2, 4)
-        load_d(0, 2, 4)
-        load_d(1, 0, 4)
-        for l in range(4):
+        def load_s(queue):
+            for q in range(4):
+                queue.dma_start(
+                    out=sraw32[32 * q : 32 * q + 4, :, :],
+                    in_=scales32[:, 4 * q : 4 * q + 4, :].rearrange("g r n -> r g n"),
+                )
+
+        def load_x1(l):
             nc.sync.dma_start(out=x1[l][:], in_=resid[512 + 128 * l : 640 + 128 * l, :])
+
+        def load_w():
+            for vg in range(VG):
+                nc.sync.dma_start(out=wraw[vg:P:32, :], in_=weight.rearrange("(v q n) -> v q n", v=VG, q=4)[vg])
+
+        if LOADS == 0:
+            load_s(nc.scalar)
+            load_x0(0, 0, 2)
+            load_x0(0, 2, 4)
+            load_x0(1, 0, 2)
+            load_d(0, 0, 2)
+            load_w()
+            load_x0(1, 2, 4)
+            load_d(0, 2, 4)
+            load_d(1, 0, 4)
+        elif LOADS == 1:
+            load_x0(0, 0, 2)
+            load_x0(0, 2, 4)
+            load_s(nc.sync)
+            load_x0(1, 0, 2)
+            load_d(2, 0, 2)
+            load_x0(1, 2, 4)
+            load_w()
+            load_d(2, 2, 4)
+        elif LOADS == 2:
+            load_x0(0, 0, 2)
+            load_x0(0, 2, 4)
+            load_s(nc.sync)
+            load_x0(1, 0, 2)
+            load_d(0, 0, 2)
+            load_x0(1, 2, 4)
+            load_w()
+            load_d(0, 2, 4)
+            load_d(1, 0, 4)
+        elif LOADS == 3:
+            load_x0(0, 0, 2)
+            load_x0(0, 2, 4)
+            load_s(nc.sync)
+            load_x0(1, 0, 2)
+            load_d(2, 0, 1)
+            load_d(2, 1, 2)
+            load_x0(1, 2, 4)
+            load_w()
+            load_d(2, 2, 4)
+        elif LOADS == 4:
+            load_x0(0, 0, 2)
+            load_x0(0, 2, 4)
+            load_s(nc.sync)
+            load_x0(1, 0, 2)
+            load_d(2, 0, 1)
+            load_x0(1, 2, 4)
+            load_d(2, 1, 2)
+            load_w()
+            load_d(2, 2, 4)
+        elif LOADS == 5:
+            load_x0(0, 0, 2)
+            load_x0(0, 2, 4)
+            load_s(nc.sync)
+            load_x0(1, 0, 2)
+            load_d(2, 0, 2)
+            load_x0(1, 2, 4)
+            load_w()
+            load_d(2, 2, 4)
+        for l in range(4):
+            load_x1(l)
         mview = member.rearrange("(v m t i) w -> v i m t w", v=VG, t=4, i=4)
         for vg in range(VG):
             for i in range(4):
                 nc.sync.dma_start(out=mraw[i:P:4, vg, :, :], in_=mview[vg, i])
+        nc.sync.dma_start(
+            out=vraw[0:P:32, :].rearrange("q (c s) -> q c s", s=32), in_=inv_var.rearrange("(c q s) -> q c s", q=4, s=32)
+        )
         nc.scalar.activation(out=dummy[:], in_=dummy[:], func=ACT.Sqrt)
 
         xs = {}
@@ -160,8 +241,8 @@ def tile_skat_gene_scan_s9_kernel(tc, resid, dosage_words, dosage_scales, weight
             for g in (2 * k, 2 * k + 1):
                 bank = psum.tile([P, 2, 2, P], F32, name="tb", tag="tr")
                 tbank[h, g, pair] = bank
-            for l in range(2):
-                for g in (2 * k, 2 * k + 1):
+            for g in (2 * k, 2 * k + 1):
+                for l in range(2):
                     for u in range(2):
                         s = xs[h, 2 * pair + l, k]
                         if len(s.shape) == 2:
@@ -196,10 +277,10 @@ def tile_skat_gene_scan_s9_kernel(tc, resid, dosage_words, dosage_scales, weight
             src = draw[:, g, 1024 * vg : 1024 * (vg + 1)].bitcast(I32).rearrange("p (m t i) -> p t m i", t=4, i=2)
             nc.vector.tensor_copy(out=dst, in_=src)
 
-        def permute_scales():
+        def permute_scales(lo, hi):
             src = sraw32.rearrange("p g n -> p (g n)").rearrange("p (c m t) -> p c t m", c=8, t=4)
             dst = sperm[:].rearrange("p c n -> p (c n)").bitcast(I32).rearrange("p (c t m) -> p c t m", c=8, t=4)
-            nc.vector.tensor_copy(out=dst, in_=src)
+            nc.vector.tensor_copy(out=dst[:, lo:hi], in_=src[:, lo:hi])
 
         acc = {}
 
@@ -225,19 +306,25 @@ def tile_skat_gene_scan_s9_kernel(tc, resid, dosage_words, dosage_scales, weight
             if t == 0:
                 sq = work.tile([P, 4, 512], BF16, name="hsq", tag="hsq", bufs=2, align_bytes=64)
                 hsq[h, vg] = sq
-            nc.scalar.activation(
-                out=hsq[h, vg][:, t, :],
-                in_=acc[h, vg, t][:],
-                func=ACT.Square,
-                scale=rootw[:, 4 * vg + t : 4 * vg + t + 1],
-            )
+            parts = SPLIT if (h, vg, t) == (1, 1, 3) and SPLIT else 1
+            for q in range(parts):
+                cols = slice(512 // parts * q, 512 // parts * (q + 1))
+                nc.scalar.activation(
+                    out=hsq[h, vg][:, t, cols],
+                    in_=acc[h, vg, t][:, cols],
+                    func=ACT.Square,
+                    scale=rootw[:, 4 * vg + t : 4 * vg + t + 1],
+                )
 
         hg = {}
 
         def interleave_h(h, vg, lo, hi):
             dst = work.tile([P, hi - lo, 4], BF16, name="hg", tag="hg%d" % (hi - lo), bufs=2, align_bytes=64)
             hg[h, vg, lo] = dst
-            nc.vector.tensor_copy(out=dst[:], in_=hsq[h, vg][:, :, lo:hi].rearrange("p t r -> p r t"))
+            nc.vector.tensor_copy(
+                out=dst[:].rearrange("p (c i) t -> p c t i", i=4),
+                in_=hsq[h, vg][:, :, lo:hi].rearrange("p t (c i) -> p c t i", i=4),
+            )
 
         def quantize_h(h, vg, lo, hi):
             nc.vector.quantize_mx(
@@ -285,38 +372,51 @@ def tile_skat_gene_scan_s9_kernel(tc, resid, dosage_words, dosage_scales, weight
         def store(h, l, engine):
             o = outs.tile([P, N], F32, name="o", tag="o", align_bytes=64)
             tile_no = 4 * h + l
-            factor = wcol[:, 8 + tile_no : 9 + tile_no]
+            factor = vcol[:, tile_no : tile_no + 1]
             if engine == "S":
                 nc.scalar.activation(out=o[:], in_=obank[h, l][:], func=ACT.Copy, scale=factor)
             else:
                 nc.vector.tensor_scalar(out=o[:], in0=obank[h, l][:], scalar1=factor, scalar2=None, op0=ALU.mult)
             nc.sync.dma_start(out=out[128 * tile_no : 128 * (tile_no + 1), :], in_=o[:])
 
-        def weight_transpose():
-            nc.vector.tensor_copy(out=wrow32[:], in_=wrow[:])
-            bank = psum.tile([P, 512], F32, name="wb", tag="tr")
-            nc.tensor.transpose(bank[:, 0:P], wrow32[:], ident[:])
-            tbank["w"] = bank
+        def weight_slots():
+            nc.vector.tensor_copy(
+                out=wslot[:].rearrange("p (t m i) -> p t m i", t=4, i=4),
+                in_=wraw[:].rearrange("p (m t i) -> p t m i", t=4, i=4),
+            )
 
-        def weight_copy():
-            nc.vector.tensor_copy(out=wcol[:], in_=tbank["w"][:, 0:16])
+        def weight_turn():
+            nc.vector.transpose(out=wturn[:], in_=wslot[:])
 
-        def weight_roots():
-            w = wcol[:, 0:8]
-            nc.vector.scalar_tensor_tensor(out=absw[:], in0=w, scalar=-1.0, in1=w, op0=ALU.mult, op1=ALU.max)
-            nc.vector.tensor_scalar(out=sgn[:], in0=w, scalar1=0.0, scalar2=2.0, op0=ALU.is_ge, op1=ALU.mult)
+        def factor_turn():
+            nc.vector.transpose(out=vturn[:], in_=vraw[:])
+            nc.vector.tensor_copy(out=vcol[:], in_=vturn[:].rearrange("p (c r) -> p c r", r=32)[:, :, 0])
+
+        def by_slot(tile):
+            return tile[:].rearrange("p (v t) -> p t v", v=VG)
+
+        def weight_parts():
+            w = wturn[:].rearrange("p (t r) -> p t r", r=32)[:, :, 0:VG]
+            nc.vector.scalar_tensor_tensor(out=by_slot(absw), in0=w, scalar=-1.0, in1=w, op0=ALU.mult, op1=ALU.max)
+            nc.vector.tensor_scalar(out=by_slot(sgn), in0=w, scalar1=0.0, scalar2=2.0, op0=ALU.is_ge, op1=ALU.mult)
+
+        def weight_root():
             nc.scalar.activation(out=root[:], in_=absw[:], func=ACT.Sqrt)
 
-        def refine_roots():
-            nc.vector.tensor_scalar(out=rclamp[:], in0=root[:], scalar1=1e-20, scalar2=None, op0=ALU.max)
-            nc.vector.tensor_scalar(out=sgn16[:], in0=sgn[:], scalar1=1.0, scalar2=None, op0=ALU.subtract)
-            nc.vector.reciprocal(out=rinv[:], in_=rclamp[:])
-            nc.vector.scalar_tensor_tensor(out=quot[:], in0=rinv[:], scalar=0.5, in1=absw[:], op0=ALU.mult, op1=ALU.mult)
-            nc.vector.scalar_tensor_tensor(out=rootw[:], in0=root[:], scalar=0.5, in1=quot[:], op0=ALU.mult, op1=ALU.add)
+        def refine_root(step):
+            if step == 0:
+                nc.vector.tensor_scalar(out=rclamp[:], in0=root[:], scalar1=1e-20, scalar2=None, op0=ALU.max)
+                nc.vector.tensor_scalar(out=sgn16[:], in0=sgn[:], scalar1=1.0, scalar2=None, op0=ALU.subtract)
+            elif step == 1:
+                nc.vector.reciprocal(out=rinv[:], in_=rclamp[:])
+            elif step == 2:
+                nc.vector.scalar_tensor_tensor(out=quot[:], in0=rinv[:], scalar=0.5, in1=absw[:], op0=ALU.mult, op1=ALU.mult)
+            else:
+                nc.vector.scalar_tensor_tensor(out=rootw[:], in0=root[:], scalar=0.5, in1=quot[:], op0=ALU.mult, op1=ALU.add)
 
         def evacuate_pair(h, k, pair):
             for g in (2 * k, 2 * k + 1):
-                evacuate(h, g, pair, EV[h, pair][g % 2])
+                evacuate(h, g, pair, EV[h, k, pair][g % 2])
 
         open_acc(0, 0)
 
@@ -340,71 +440,156 @@ def tile_skat_gene_scan_s9_kernel(tc, resid, dosage_words, dosage_scales, weight
         evacuate_pair(0, 0, 0)
         transposes(0, 0, 1)
         evacuate_pair(0, 0, 1)
+        warm_up(D1)
         quantize_x(0, 0, 0, 256)
         quantize_x(0, 1, 0, 256)
-        permute_scales()
-        permute_d(0, 0)
+        permute_scales(0, 4)
+        if SC == 0:
+            permute_scales(4, 8)
         transposes(0, 1, 0)
         evacuate_pair(0, 1, 0)
         quantize_x(0, 0, 256, 512)
-        permute_d(0, 1)
+        permute_d(0, 0)
         quantize_x(0, 1, 256, 512)
+        permute_d(0, 1)
+        warm_up(D2)
         for t in range(4):
             stage1(0, 0, t, 0)
-        weight_transpose()
-        quantize_x(0, 2, 0, 256)
-        quantize_x(0, 3, 0, 256)
-        permute_d(0, 2)
-        permute_d(0, 3)
-        weight_copy()
-        weight_roots()
+        if SC == 1:
+            permute_scales(4, 8)
+        if PD == 1:
+            permute_d(0, 1)
+        if WP == 0:
+            quantize_x(0, 2, 0, 256)
+            weight_slots()
+            quantize_x(0, 3, 0, 256)
+            weight_turn()
+            permute_d(0, 2)
+            weight_parts()
+            permute_d(0, 3)
+        else:
+            weight_slots()
+            quantize_x(0, 2, 0, 256)
+            weight_turn()
+            quantize_x(0, 3, 0, 256)
+            weight_parts()
+            permute_d(0, 2)
+            permute_d(0, 3)
         transposes(0, 1, 1)
         evacuate_pair(0, 1, 1)
-        refine_roots()
+        weight_root()
         for t in range(4):
             stage1(0, 0, t, 1)
-        quantize_x(0, 2, 256, 512)
-        quantize_x(0, 3, 256, 512)
-        reorder_x1(0)
-        reorder_x1(1)
+        if RP == 0:
+            quantize_x(0, 2, 256, 512)
+            quantize_x(0, 3, 256, 512)
+            refine_root(0)
+            permute_d(1, 0)
+            refine_root(1)
+            permute_d(1, 1)
+            refine_root(2)
+            permute_d(1, 2)
+            refine_root(3)
+            permute_d(1, 3)
+            reorder_x1(0)
+            reorder_x1(1)
+        else:
+            quantize_x(0, 2, 256, 512)
+            quantize_x(0, 3, 256, 512)
+            refine_root(0)
+            reorder_x1(0)
+            refine_root(1)
+            permute_d(1, 0)
+            refine_root(2)
+            permute_d(1, 1)
+            refine_root(3)
+            reorder_x1(1)
+            permute_d(1, 2)
+            permute_d(1, 3)
         for t in range(4):
             for g in range(2, 4):
                 stage1(0, 0, t, g)
             square(0, 0, t)
 
-        for g in range(G):
-            permute_d(1, g)
+        def block(t):
+            for g in range(G):
+                stage1(0, 1, t, g)
+            square(0, 1, t)
+
+        def turn(pair):
+            for k in range(2):
+                transposes(1, k, pair)
+            for k in range(2):
+                evacuate_pair(1, k, pair)
+
         open_acc(0, 1)
-        transposes(1, 0, 0)
-        transposes(1, 1, 0)
-        evacuate_pair(1, 0, 0)
-        evacuate_pair(1, 1, 0)
-        reorder_x1(2)
-        reorder_x1(3)
-        for t in range(2):
+        if MID == 0:
+            turn(0)
+            reorder_x1(2)
+            reorder_x1(3)
+            block(0)
+            block(1)
+            interleave_h(0, 0, 0, 512)
             for g in range(G):
-                stage1(0, 1, t, g)
-            square(0, 1, t)
-        interleave_h(0, 0, 0, 512)
-        for g in range(G):
-            quantize_x(1, g, 0, 256)
-        quantize_h(0, 0, 0, 512)
-        transposes(1, 0, 1)
-        transposes(1, 1, 1)
-        evacuate_pair(1, 0, 1)
-        evacuate_pair(1, 1, 1)
-        for g in range(G):
-            quantize_x(1, g, 256, 512)
-        for t in range(2, 4):
+                quantize_x(1, g, 0, 256)
+            quantize_h(0, 0, 0, 512)
+            turn(1)
             for g in range(G):
-                stage1(0, 1, t, g)
-            square(0, 1, t)
-        interleave_m(0)
+                quantize_x(1, g, 256, 512)
+            block(2)
+            block(3)
+        elif MID == 1:
+            block(0)
+            turn(0)
+            reorder_x1(2)
+            reorder_x1(3)
+            block(1)
+            for g in range(G):
+                quantize_x(1, g, 0, 256)
+            turn(1)
+            interleave_h(0, 0, 0, 512)
+            for g in range(G):
+                quantize_x(1, g, 256, 512)
+            quantize_h(0, 0, 0, 512)
+            block(2)
+            block(3)
+        elif MID == 2:
+            block(0)
+            turn(0)
+            interleave_h(0, 0, 0, 512)
+            reorder_x1(2)
+            reorder_x1(3)
+            block(1)
+            block(2)
+            for g in range(G):
+                quantize_x(1, g, 0, 256)
+            quantize_h(0, 0, 0, 512)
+            turn(1)
+            for g in range(G):
+                quantize_x(1, g, 256, 512)
+            block(3)
+        elif MID == 3:
+            block(0)
+            block(1)
+            turn(0)
+            reorder_x1(2)
+            reorder_x1(3)
+            interleave_h(0, 0, 0, 512)
+            for g in range(G):
+                quantize_x(1, g, 0, 256)
+            block(2)
+            turn(1)
+            quantize_h(0, 0, 0, 512)
+            for g in range(G):
+                quantize_x(1, g, 256, 512)
+            block(3)
         interleave_h(0, 1, 0, 512)
-        quantize_m(0)
-        interleave_m(1)
+        interleave_m(0)
         quantize_h(0, 1, 0, 512)
+        interleave_m(1)
+        quantize_m(0)
         quantize_m(1)
+        factor_turn()
 
         open_acc(1, 0)
         for g in range(2):
@@ -421,22 +606,53 @@ def tile_skat_gene_scan_s9_kernel(tc, resid, dosage_words, dosage_scales, weight
             for g in range(G):
                 stage1(1, 1, t, g)
             square(1, 1, t)
-            if t in (1, 2):
-                for vg in range(VG):
-                    stage2(0, t - 1, vg)
-                store(0, t - 1, "S")
+            if t in WEAVE:
+                for l in range(WEAVE[t][0], WEAVE[t][1]):
+                    for vg in range(VG):
+                        stage2(0, l, vg)
+                    store(0, l, "S")
 
-        for l in range(2, 4):
-            for vg in range(VG):
-                stage2(0, l, vg)
-        interleave_h(1, 1, 0, 256)
-        interleave_h(1, 1, 256, 512)
-        quantize_h(1, 1, 0, 256)
-        quantize_h(1, 1, 256, 512)
-        for l in range(2, 4):
-            store(0, l, "S")
-        for l in range(4):
-            stage2(1, l, 0)
-        for l in range(4):
-            stage2(1, l, 1)
-            store(1, l, "V" if l % 2 else "S")
+        if S2O == 0:
+            for l in range(EARLY, 4):
+                for vg in range(VG):
+                    stage2(0, l, vg)
+            interleave_h(1, 1, 0, 256)
+            quantize_h(1, 1, 0, 256)
+            interleave_h(1, 1, 256, 512)
+            quantize_h(1, 1, 256, 512)
+            for l in range(EARLY, 4):
+                store(0, l, "S")
+            for l in range(4):
+                stage2(1, l, 0)
+            for l in range(4):
+                stage2(1, l, 1)
+                store(1, l, "V" if l % 2 else "S")
+        else:
+            lo, hi = TP
+            for l in range(EARLY, LATE):
+                for vg in range(VG):
+                    stage2(0, l, vg)
+            if TP[0] == 256:
+                interleave_h(1, 1, 0, 256)
+                quantize_h(1, 1, 0, 256)
+            else:
+                interleave_h(1, 1, 0, 128)
+                interleave_h(1, 1, 128, 256)
+                quantize_h(1, 1, 0, 128)
+                quantize_h(1, 1, 128, 256)
+            interleave_h(1, 1, 256, 512)
+            quantize_h(1, 1, 256, 512)
+            for l in range(EARLY, LATE):
+                store(0, l, "S")
+            for l in range(4):
+                stage2(1, l, 0)
+            for l in range(2):
+                stage2(1, l, 1)
+                store(1, l, "S")
+            for l in range(LATE, 4):
+                for vg in range(VG):
+                    stage2(0, l, vg)
+                store(0, l, E3)
+            for l in range(2, 4):
+                stage2(1, l, 1)
+                store(1, l, E2[l - 2])

from contextlib import ExitStack

import concourse.mybir as mybir
from concourse.masks import make_identity

T, K, V, N = 1024, 2048, 1024, 512

FLOPS = 2 * T * K * V + 2 * T * V * N

F32 = mybir.dt.float32
BF16 = mybir.dt.bfloat16
U32 = mybir.dt.uint32
I32 = mybir.dt.int32
U8 = mybir.dt.uint8
E4M3X4 = mybir.dt.float8_e4m3fn_x4
E5M2X4 = mybir.dt.float8_e5m2_x4
E2M1X4 = mybir.dt.float4_e2m1fn_x4
ACT = mybir.ActivationFunctionType
ALU = mybir.AluOpType

P = 128
G = K // 512
H = 2
VG = 2
R0 = ["NNNN", "NNNN"]
R1 = "VVVV"
WARM = 4
D1 = 0
D2 = 0
MID = 1
S2O = 0
LATE = 3
TP = (256, 256)
E3 = "V"
E2 = "SV"
PD = 0
WP = 0
RP = 0
SC = 1
EV = {(0, 0, 0): "SS", (0, 0, 1): "SS", (0, 1, 0): "SS", (0, 1, 1): "SS", (1, 0, 0): "SS", (1, 0, 1): "SS", (1, 1, 0): "SS", (1, 1, 1): "SS"}
WEAVE = {2: (0, 1)}
EARLY = 1
TAIL = 1
LOADS = 2
SPLIT = 2
TS = "SSSS"


def tile_skat_gene_scan_s9_kernel(tc, resid, dosage_words, dosage_scales, weight, member, inv_var, out):
    nc = tc.nc
    with ExitStack() as ctx:
        keep = ctx.enter_context(tc.tile_pool(name="keep", bufs=1))
        work = ctx.enter_context(tc.tile_pool(name="work", bufs=4))
        outs = ctx.enter_context(tc.tile_pool(name="outs", bufs=8))
        psum = ctx.enter_context(tc.psum_pool(name="psum", bufs=4))
        ctx.enter_context(tc.manual_schedule())

        def keep_tile(shape, dtype, name):
            return keep.tile(shape, dtype, name=name, tag=name, align_bytes=64)

        ident = keep_tile([P, P], F32, "ident")
        sraw = keep_tile([P, G, V], U8, "sraw")
        sperm = keep_tile([P, G * VG, 512], U8, "sperm")
        wraw = keep_tile([P, P], BF16, "wraw")
        wslot = keep_tile([P, P], BF16, "wslot")
        wturn = keep_tile([P, P], BF16, "wturn")
        vraw = keep_tile([P, 256], BF16, "vraw")
        vturn = keep_tile([P, 256], BF16, "vturn")
        vcol = keep_tile([P, 8], F32, "vcol")
        sgn = keep_tile([P, 8], F32, "sgn")
        sgn16 = keep_tile([P, 8], BF16, "sgn16")
        absw = keep_tile([P, 8], F32, "absw")
        root = keep_tile([P, 8], F32, "root")
        rclamp = keep_tile([P, 8], F32, "rclamp")
        rinv = keep_tile([P, 8], F32, "rinv")
        quot = keep_tile([P, 8], F32, "quot")
        rootw = keep_tile([P, 8], F32, "rootw")
        dummy = keep_tile([P, 1], F32, "dummy")
        warm = keep_tile([P, 512], BF16, "warm")
        warm4 = keep_tile([P, 512], U32, "warm4")
        warm4s = keep_tile([P, 512], U8, "warm4s")
        warm5 = keep_tile([P, 128], U32, "warm5")
        warm5s = keep_tile([P, 128], U8, "warm5s")
        draw = keep_tile([P, G, 2 * V], U8, "draw")
        dperm = keep_tile([P, VG, G, 1024], U8, "dperm")
        mraw = keep_tile([P, VG, 4, N], BF16, "mraw")
        x0 = [keep_tile([P, 4, 1024], BF16, "x0%d" % k) for k in range(2)]
        x1 = [keep_tile([P, 2048], BF16, "x1%d" % l) for l in range(4)]
        rcode = {}
        rscale = {}
        for h in range(H):
            for g in range(G):
                rcode[h, g] = keep_tile([P, 512], U32, "rc%d%d" % (h, g))
                rscale[h, g] = keep_tile([P, 512], U8, "rs%d%d" % (h, g))
        hcode = {}
        hscale = {}
        for h in range(H):
            for vg in range(VG):
                hcode[h, vg] = keep_tile([P, 512], U32, "hc%d%d" % (h, vg))
                hscale[h, vg] = keep_tile([P, 512], U8, "hs%d%d" % (h, vg))
        mcode = [keep_tile([P, N], U32, "mc%d" % vg) for vg in range(VG)]
        mscale = [keep_tile([P, N], U8, "ms%d" % vg) for vg in range(VG)]

        nc.vector.memset(warm[:].bitcast(I32), 0)
        nc.gpsimd.memset(warm4[:, 128:512], 0)
        nc.gpsimd.memset(warm4s[:, 128:512].bitcast(I32), 0)
        nc.vector.memset(sraw[:].rearrange("p g n -> p (g n)").bitcast(I32), 0)
        nc.vector.memset(dummy[:], 0.0)
        nc.vector.quantize_mx(out=warm5[:].bitcast(E5M2X4), scales=warm5s[:], in_=warm[:])
        nc.vector.quantize_mx(out=warm4[:, 0:128].bitcast(E4M3X4), scales=warm4s[:, 0:128], in_=warm[:])
        nc.vector.memset(wraw[:].bitcast(I32), 0)
        nc.vector.memset(vraw[:].bitcast(I32), 0)
        make_identity(nc, ident[:])

        def load_x0(k, lo, hi):
            nc.sync.dma_start(
                out=x0[k][:, lo:hi, :],
                in_=resid[128 * lo : 128 * hi, 1024 * k : 1024 * (k + 1)].rearrange("(l p) k -> p l k", p=P),
            )

        words32 = dosage_words.bitcast(I32)
        scales32 = dosage_scales.bitcast(I32)
        sraw32 = sraw[:].rearrange("p g n -> p (g n)").bitcast(I32).rearrange("p (g n) -> p g n", g=G)
        draw32 = draw[:].rearrange("p g n -> p (g n)").bitcast(I32).rearrange("p (g n) -> p g n", g=G)
        def load_d(vg, lo, hi):
            cols = slice(256 * vg, 256 * (vg + 1)) if vg < 2 else slice(0, 512)
            nc.sync.dma_start(out=draw32[:, lo:hi, cols], in_=words32[lo:hi, :, cols].rearrange("g p n -> p g n"))

        def load_s(queue):
            for q in range(4):
                queue.dma_start(
                    out=sraw32[32 * q : 32 * q + 4, :, :],
                    in_=scales32[:, 4 * q : 4 * q + 4, :].rearrange("g r n -> r g n"),
                )

        def load_x1(l):
            nc.sync.dma_start(out=x1[l][:], in_=resid[512 + 128 * l : 640 + 128 * l, :])

        def load_w():
            for vg in range(VG):
                nc.sync.dma_start(out=wraw[vg:P:32, :], in_=weight.rearrange("(v q n) -> v q n", v=VG, q=4)[vg])

        if LOADS == 0:
            load_s(nc.scalar)
            load_x0(0, 0, 2)
            load_x0(0, 2, 4)
            load_x0(1, 0, 2)
            load_d(0, 0, 2)
            load_w()
            load_x0(1, 2, 4)
            load_d(0, 2, 4)
            load_d(1, 0, 4)
        elif LOADS == 1:
            load_x0(0, 0, 2)
            load_x0(0, 2, 4)
            load_s(nc.sync)
            load_x0(1, 0, 2)
            load_d(2, 0, 2)
            load_x0(1, 2, 4)
            load_w()
            load_d(2, 2, 4)
        elif LOADS == 2:
            load_x0(0, 0, 2)
            load_x0(0, 2, 4)
            load_s(nc.sync)
            load_x0(1, 0, 2)
            load_d(0, 0, 2)
            load_x0(1, 2, 4)
            load_w()
            load_d(0, 2, 4)
            load_d(1, 0, 4)
        elif LOADS == 3:
            load_x0(0, 0, 2)
            load_x0(0, 2, 4)
            load_s(nc.sync)
            load_x0(1, 0, 2)
            load_d(2, 0, 1)
            load_d(2, 1, 2)
            load_x0(1, 2, 4)
            load_w()
            load_d(2, 2, 4)
        elif LOADS == 4:
            load_x0(0, 0, 2)
            load_x0(0, 2, 4)
            load_s(nc.sync)
            load_x0(1, 0, 2)
            load_d(2, 0, 1)
            load_x0(1, 2, 4)
            load_d(2, 1, 2)
            load_w()
            load_d(2, 2, 4)
        elif LOADS == 5:
            load_x0(0, 0, 2)
            load_x0(0, 2, 4)
            load_s(nc.sync)
            load_x0(1, 0, 2)
            load_d(2, 0, 2)
            load_x0(1, 2, 4)
            load_w()
            load_d(2, 2, 4)
        for l in range(4):
            load_x1(l)
        mview = member.rearrange("(v m t i) w -> v i m t w", v=VG, t=4, i=4)
        for vg in range(VG):
            for i in range(4):
                nc.sync.dma_start(out=mraw[i:P:4, vg, :, :], in_=mview[vg, i])
        nc.sync.dma_start(
            out=vraw[0:P:32, :].rearrange("q (c s) -> q c s", s=32), in_=inv_var.rearrange("(c q s) -> q c s", q=4, s=32)
        )
        nc.scalar.activation(out=dummy[:], in_=dummy[:], func=ACT.Sqrt)

        xs = {}

        def reorder_x0(k, l):
            if R0[k][l] == "N":
                flat = x0[k][:, l, :].bitcast(F32)
                xs[0, l, k] = flat
                return
            tile = work.tile([P, 2, 2, P], F32, name="xs0", tag="xs0", bufs=8, align_bytes=64)
            xs[0, l, k] = tile
            src = x0[k][:, l, :].bitcast(F32)
            cp = nc.vector.tensor_copy if R0[k][l] == "V" else nc.scalar.copy
            cp(out=tile[:], in_=src.rearrange("p (g i u) -> p g u i", u=2, i=P))

        def reorder_x1(l):
            if R1[l] == "N":
                flat = x1[l][:].bitcast(F32)
                xs[1, l, 0] = flat[:, 0:512]
                xs[1, l, 1] = flat[:, 512:1024]
                return
            tile = work.tile([P, 4, 2, P], F32, name="xs1", tag="xs1", bufs=4, align_bytes=64)
            src = x1[l][:].bitcast(F32)
            cp = nc.vector.tensor_copy if R1[l] == "V" else nc.scalar.copy
            cp(out=tile[:], in_=src.rearrange("p (g i u) -> p g u i", u=2, i=P))
            xs[1, l, 0] = tile[:, 0:2, :, :]
            xs[1, l, 1] = tile[:, 2:4, :, :]

        tbank = {}

        def transposes(h, k, pair):
            for g in (2 * k, 2 * k + 1):
                bank = psum.tile([P, 2, 2, P], F32, name="tb", tag="tr")
                tbank[h, g, pair] = bank
            for g in (2 * k, 2 * k + 1):
                for l in range(2):
                    for u in range(2):
                        s = xs[h, 2 * pair + l, k]
                        if len(s.shape) == 2:
                            s = s[:, 256 * (g % 2) + u : 256 * (g % 2) + 256 : 2]
                        else:
                            s = s[:, g % 2, u, :]
                        nc.tensor.transpose(tbank[h, g, pair][:, l, u, :], s, ident[:])

        xg = {}

        def evacuate(h, g, pair, engine):
            if pair == 0:
                tile = work.tile([P, 512, 4], BF16, name="xg", tag="xg", bufs=8, align_bytes=64)
                xg[h, g] = tile
            cols = xg[h, g][:, 256 * pair : 256 * (pair + 1), :]
            o = cols.rearrange("p r t -> p (r t)").bitcast(F32).rearrange("p (l r u) -> p l r u", l=2, u=2)
            i = tbank[h, g, pair][:].rearrange("p l u r -> p l r u")
            if engine == "S":
                nc.scalar.copy(out=o, in_=i)
            else:
                nc.vector.tensor_copy(out=o, in_=i)

        def quantize_x(h, g, lo, hi):
            nc.vector.quantize_mx(
                out=rcode[h, g][:, lo:hi].bitcast(E4M3X4),
                scales=rscale[h, g][:, lo:hi],
                in_=xg[h, g][:, lo:hi, :].rearrange("p r t -> p (r t)"),
            )

        def permute_d(vg, g):
            dst = dperm[:, vg, g, :].bitcast(I32).rearrange("p (t m i) -> p t m i", t=4, i=2)
            src = draw[:, g, 1024 * vg : 1024 * (vg + 1)].bitcast(I32).rearrange("p (m t i) -> p t m i", t=4, i=2)
            nc.vector.tensor_copy(out=dst, in_=src)

        def permute_scales(lo, hi):
            src = sraw32.rearrange("p g n -> p (g n)").rearrange("p (c m t) -> p c t m", c=8, t=4)
            dst = sperm[:].rearrange("p c n -> p (c n)").bitcast(I32).rearrange("p (c t m) -> p c t m", c=8, t=4)
            nc.vector.tensor_copy(out=dst[:, lo:hi], in_=src[:, lo:hi])

        acc = {}

        def open_acc(h, vg):
            for t in range(4):
                bank = psum.tile([P, 512], F32, name="acc", tag="acc")
                acc[h, vg, t] = bank

        def stage1(h, vg, t, g):
            nc.tensor.matmul_mx(
                out=acc[h, vg, t][:],
                lhsT=dperm[:, vg, g, 256 * t : 256 * (t + 1)].bitcast(E2M1X4),
                lhsT_scale=sperm[:, VG * g + vg, 128 * t : 128 * (t + 1)],
                rhs=rcode[h, g][:].bitcast(E4M3X4),
                rhs_scale=rscale[h, g][:],
                start=(g == 0),
                stop=(g == G - 1),
            )

        hsq = {}

        def square(h, vg, t):
            if t == 0:
                sq = work.tile([P, 4, 512], BF16, name="hsq", tag="hsq", bufs=2, align_bytes=64)
                hsq[h, vg] = sq
            parts = SPLIT if (h, vg, t) == (1, 1, 3) and SPLIT else 1
            for q in range(parts):
                cols = slice(512 // parts * q, 512 // parts * (q + 1))
                nc.scalar.activation(
                    out=hsq[h, vg][:, t, cols],
                    in_=acc[h, vg, t][:, cols],
                    func=ACT.Square,
                    scale=rootw[:, 4 * vg + t : 4 * vg + t + 1],
                )

        hg = {}

        def interleave_h(h, vg, lo, hi):
            dst = work.tile([P, hi - lo, 4], BF16, name="hg", tag="hg%d" % (hi - lo), bufs=2, align_bytes=64)
            hg[h, vg, lo] = dst
            nc.vector.tensor_copy(
                out=dst[:].rearrange("p (c i) t -> p c t i", i=4),
                in_=hsq[h, vg][:, :, lo:hi].rearrange("p t (c i) -> p c t i", i=4),
            )

        def quantize_h(h, vg, lo, hi):
            nc.vector.quantize_mx(
                out=hcode[h, vg][:, lo:hi].bitcast(E5M2X4),
                scales=hscale[h, vg][:, lo:hi],
                in_=hg[h, vg, lo][:].rearrange("p r t -> p (r t)"),
            )

        mg = {}

        def interleave_m(vg):
            dst = work.tile([P, N, 4], BF16, name="mg", tag="mg", bufs=2, align_bytes=64)
            mg[vg] = dst
            nc.vector.tensor_tensor(
                out=dst[:],
                in0=mraw[:, vg, :, :].rearrange("p t w -> p w t"),
                in1=sgn16[:, 4 * vg : 4 * vg + 4].unsqueeze(1).to_broadcast([P, N, 4]),
                op=ALU.mult,
            )

        def quantize_m(vg):
            nc.vector.quantize_mx(
                out=mcode[vg][:].bitcast(E4M3X4),
                scales=mscale[vg][:],
                in_=mg[vg][:].rearrange("p w t -> p (w t)"),
            )

        obank = {}

        def stage2(h, l, vg):
            if vg == 0:
                bank = psum.tile([P, N], F32, name="ob", tag="tr" if h == 0 else "acc")
                obank[h, l] = bank
            cols = slice(128 * l, 128 * (l + 1))
            nc.tensor.matmul_mx(
                out=obank[h, l][:],
                lhsT=hcode[h, vg][:, cols].bitcast(E5M2X4),
                lhsT_scale=hscale[h, vg][:, cols],
                rhs=mcode[vg][:].bitcast(E4M3X4),
                rhs_scale=mscale[vg][:],
                start=(vg == 0),
                stop=(vg == VG - 1),
            )

        def store(h, l, engine):
            o = outs.tile([P, N], F32, name="o", tag="o", align_bytes=64)
            tile_no = 4 * h + l
            factor = vcol[:, tile_no : tile_no + 1]
            if engine == "S":
                nc.scalar.activation(out=o[:], in_=obank[h, l][:], func=ACT.Copy, scale=factor)
            else:
                nc.vector.tensor_scalar(out=o[:], in0=obank[h, l][:], scalar1=factor, scalar2=None, op0=ALU.mult)
            nc.sync.dma_start(out=out[128 * tile_no : 128 * (tile_no + 1), :], in_=o[:])

        def weight_slots():
            nc.vector.tensor_copy(
                out=wslot[:].rearrange("p (t m i) -> p t m i", t=4, i=4),
                in_=wraw[:].rearrange("p (m t i) -> p t m i", t=4, i=4),
            )

        def weight_turn():
            nc.vector.transpose(out=wturn[:], in_=wslot[:])

        def factor_turn():
            nc.vector.transpose(out=vturn[:], in_=vraw[:])
            nc.vector.tensor_copy(out=vcol[:], in_=vturn[:].rearrange("p (c r) -> p c r", r=32)[:, :, 0])

        def by_slot(tile):
            return tile[:].rearrange("p (v t) -> p t v", v=VG)

        def weight_parts():
            w = wturn[:].rearrange("p (t r) -> p t r", r=32)[:, :, 0:VG]
            nc.vector.scalar_tensor_tensor(out=by_slot(absw), in0=w, scalar=-1.0, in1=w, op0=ALU.mult, op1=ALU.max)
            nc.vector.tensor_scalar(out=by_slot(sgn), in0=w, scalar1=0.0, scalar2=2.0, op0=ALU.is_ge, op1=ALU.mult)

        def weight_root():
            nc.scalar.activation(out=root[:], in_=absw[:], func=ACT.Sqrt)

        def refine_root(step):
            if step == 0:
                nc.vector.tensor_scalar(out=rclamp[:], in0=root[:], scalar1=1e-20, scalar2=None, op0=ALU.max)
                nc.vector.tensor_scalar(out=sgn16[:], in0=sgn[:], scalar1=1.0, scalar2=None, op0=ALU.subtract)
            elif step == 1:
                nc.vector.reciprocal(out=rinv[:], in_=rclamp[:])
            elif step == 2:
                nc.vector.scalar_tensor_tensor(out=quot[:], in0=rinv[:], scalar=0.5, in1=absw[:], op0=ALU.mult, op1=ALU.mult)
            else:
                nc.vector.scalar_tensor_tensor(out=rootw[:], in0=root[:], scalar=0.5, in1=quot[:], op0=ALU.mult, op1=ALU.add)

        def evacuate_pair(h, k, pair):
            for g in (2 * k, 2 * k + 1):
                evacuate(h, g, pair, EV[h, k, pair][g % 2])

        open_acc(0, 0)

        def warm_up(passes):
            for i in range(passes):
                nc.tensor.matmul_mx(
                    out=acc[0, 0, 0][:],
                    lhsT=warm5[:].bitcast(E5M2X4),
                    lhsT_scale=warm5s[:],
                    rhs=warm4[:].bitcast(E4M3X4),
                    rhs_scale=warm4s[:],
                    start=True,
                    stop=True,
                )

        warm_up(WARM)
        for k in range(2):
            for l in range(4):
                reorder_x0(k, l)
        transposes(0, 0, 0)
        evacuate_pair(0, 0, 0)
        transposes(0, 0, 1)
        evacuate_pair(0, 0, 1)
        warm_up(D1)
        quantize_x(0, 0, 0, 256)
        quantize_x(0, 1, 0, 256)
        permute_scales(0, 4)
        if SC == 0:
            permute_scales(4, 8)
        transposes(0, 1, 0)
        evacuate_pair(0, 1, 0)
        quantize_x(0, 0, 256, 512)
        permute_d(0, 0)
        quantize_x(0, 1, 256, 512)
        permute_d(0, 1)
        warm_up(D2)
        for t in range(4):
            stage1(0, 0, t, 0)
        if SC == 1:
            permute_scales(4, 8)
        if PD == 1:
            permute_d(0, 1)
        if WP == 0:
            quantize_x(0, 2, 0, 256)
            weight_slots()
            quantize_x(0, 3, 0, 256)
            weight_turn()
            permute_d(0, 2)
            weight_parts()
            permute_d(0, 3)
        else:
            weight_slots()
            quantize_x(0, 2, 0, 256)
            weight_turn()
            quantize_x(0, 3, 0, 256)
            weight_parts()
            permute_d(0, 2)
            permute_d(0, 3)
        transposes(0, 1, 1)
        evacuate_pair(0, 1, 1)
        weight_root()
        for t in range(4):
            stage1(0, 0, t, 1)
        if RP == 0:
            quantize_x(0, 2, 256, 512)
            quantize_x(0, 3, 256, 512)
            refine_root(0)
            permute_d(1, 0)
            refine_root(1)
            permute_d(1, 1)
            refine_root(2)
            permute_d(1, 2)
            refine_root(3)
            permute_d(1, 3)
            reorder_x1(0)
            reorder_x1(1)
        else:
            quantize_x(0, 2, 256, 512)
            quantize_x(0, 3, 256, 512)
            refine_root(0)
            reorder_x1(0)
            refine_root(1)
            permute_d(1, 0)
            refine_root(2)
            permute_d(1, 1)
            refine_root(3)
            reorder_x1(1)
            permute_d(1, 2)
            permute_d(1, 3)
        for t in range(4):
            for g in range(2, 4):
                stage1(0, 0, t, g)
            square(0, 0, t)

        def block(t):
            for g in range(G):
                stage1(0, 1, t, g)
            square(0, 1, t)

        def turn(pair):
            for k in range(2):
                transposes(1, k, pair)
            for k in range(2):
                evacuate_pair(1, k, pair)

        open_acc(0, 1)
        if MID == 0:
            turn(0)
            reorder_x1(2)
            reorder_x1(3)
            block(0)
            block(1)
            interleave_h(0, 0, 0, 512)
            for g in range(G):
                quantize_x(1, g, 0, 256)
            quantize_h(0, 0, 0, 512)
            turn(1)
            for g in range(G):
                quantize_x(1, g, 256, 512)
            block(2)
            block(3)
        elif MID == 1:
            block(0)
            turn(0)
            reorder_x1(2)
            reorder_x1(3)
            block(1)
            for g in range(G):
                quantize_x(1, g, 0, 256)
            turn(1)
            interleave_h(0, 0, 0, 512)
            for g in range(G):
                quantize_x(1, g, 256, 512)
            quantize_h(0, 0, 0, 512)
            block(2)
            block(3)
        elif MID == 2:
            block(0)
            turn(0)
            interleave_h(0, 0, 0, 512)
            reorder_x1(2)
            reorder_x1(3)
            block(1)
            block(2)
            for g in range(G):
                quantize_x(1, g, 0, 256)
            quantize_h(0, 0, 0, 512)
            turn(1)
            for g in range(G):
                quantize_x(1, g, 256, 512)
            block(3)
        elif MID == 3:
            block(0)
            block(1)
            turn(0)
            reorder_x1(2)
            reorder_x1(3)
            interleave_h(0, 0, 0, 512)
            for g in range(G):
                quantize_x(1, g, 0, 256)
            block(2)
            turn(1)
            quantize_h(0, 0, 0, 512)
            for g in range(G):
                quantize_x(1, g, 256, 512)
            block(3)
        interleave_h(0, 1, 0, 512)
        interleave_m(0)
        quantize_h(0, 1, 0, 512)
        interleave_m(1)
        quantize_m(0)
        quantize_m(1)
        factor_turn()

        open_acc(1, 0)
        for g in range(2):
            for t in range(4):
                stage1(1, 0, t, g)
        for t in range(4):
            for g in range(2, 4):
                stage1(1, 0, t, g)
            square(1, 0, t)
        interleave_h(1, 0, 0, 512)
        quantize_h(1, 0, 0, 512)
        open_acc(1, 1)
        for t in range(4):
            for g in range(G):
                stage1(1, 1, t, g)
            square(1, 1, t)
            if t in WEAVE:
                for l in range(WEAVE[t][0], WEAVE[t][1]):
                    for vg in range(VG):
                        stage2(0, l, vg)
                    store(0, l, "S")

        if S2O == 0:
            for l in range(EARLY, 4):
                for vg in range(VG):
                    stage2(0, l, vg)
            interleave_h(1, 1, 0, 256)
            quantize_h(1, 1, 0, 256)
            interleave_h(1, 1, 256, 512)
            quantize_h(1, 1, 256, 512)
            for l in range(EARLY, 4):
                store(0, l, "S")
            for l in range(4):
                stage2(1, l, 0)
            for l in range(4):
                stage2(1, l, 1)
                store(1, l, "V" if l % 2 else "S")
        else:
            lo, hi = TP
            for l in range(EARLY, LATE):
                for vg in range(VG):
                    stage2(0, l, vg)
            if TP[0] == 256:
                interleave_h(1, 1, 0, 256)
                quantize_h(1, 1, 0, 256)
            else:
                interleave_h(1, 1, 0, 128)
                interleave_h(1, 1, 128, 256)
                quantize_h(1, 1, 0, 128)
                quantize_h(1, 1, 128, 256)
            interleave_h(1, 1, 256, 512)
            quantize_h(1, 1, 256, 512)
            for l in range(EARLY, LATE):
                store(0, l, "S")
            for l in range(4):
                stage2(1, l, 0)
            for l in range(2):
                stage2(1, l, 1)
                store(1, l, "S")
            for l in range(LATE, 4):
                for vg in range(VG):
                    stage2(0, l, vg)
                store(0, l, E3)
            for l in range(2, 4):
                stage2(1, l, 1)
                store(1, l, E2[l - 2])
